import numpy as np
import ml_dtypes


def mxq(x, axis, fmt="e4m3"):
    dtype, down = {"e4m3": (ml_dtypes.float8_e4m3fn, 7), "e5m2": (ml_dtypes.float8_e5m2, 14)}[fmt]
    v = np.moveaxis(np.asarray(x, np.float32).astype(ml_dtypes.bfloat16).astype(np.float64), axis, -1)
    blocks = v.reshape(v.shape[:-1] + (-1, 32))
    amax = np.abs(blocks).max(-1, keepdims=True)
    byte = np.maximum(np.where(amax > 0, np.frexp(amax)[1] - 1 + 127, 0) - down, 1)
    scale = np.exp2(byte - 127.0)
    codes = (blocks / scale).astype(np.float32).astype(dtype).astype(np.float64)
    return np.moveaxis((codes * scale).reshape(v.shape), -1, axis)


WIDE = False


def mx_kscale(k):
    if not WIDE:
        return np.ones(k)
    levels = np.array([10, -10, 5, -5, 0])
    if k % 512:
        return np.exp2(np.random.permutation(np.resize(levels, k // 32))).repeat(32)
    a = np.empty((k // 512, 16))
    for p in range(k // 512):
        a[p, :8] = np.random.permutation(np.resize(levels, 8))
        for g in range(8):
            far = levels[np.abs(levels - a[p, g]) >= 10]
            a[p, g + 8] = far[np.random.randint(len(far))]
    return np.exp2(a.ravel()).repeat(32)


def f64(x):
    return np.asarray(x).astype(np.float64)


def striped(idx):
    return np.tile(np.asarray(idx).reshape(-1, 16).T, (8, 1)).astype(np.uint16)


def unstriped(offs):
    return offs[:16].T.reshape(-1).astype(np.int64)


E2M1 = np.array([0.0, 0.5, 1.0, 1.5, 2.0, 3.0, 4.0, 6.0, -0.0, -0.5, -1.0, -1.5, -2.0, -3.0, -4.0, -6.0])


def pack_weight(w, fmt):
    k, n = w.shape
    w = f64(np.asarray(w, np.float32).astype(ml_dtypes.bfloat16)).reshape(k // 32, 32, n)
    amax = np.abs(w).max(1)
    if fmt == "e4m3":
        byte = np.frexp(amax)[1] - 1 + 127 - 7
    else:
        mant, ex = np.frexp(amax / 6.0)
        byte = np.where(mant > 0.5, ex, ex - 1) + 127
    byte = np.clip(np.where(amax > 0, byte, 1), 1, 254)
    scaled = (w * np.exp2(127.0 - byte)[:, None, :]).reshape(k, n).astype(np.float32)
    by_word = np.ascontiguousarray(scaled.reshape(k // 512, 128, 4, n).transpose(0, 1, 3, 2))
    if fmt == "e4m3":
        words = by_word.astype(ml_dtypes.float8_e4m3fn).view(np.uint8)
    else:
        c = by_word.astype(ml_dtypes.float4_e2m1fn).view(np.uint8) & 0xF
        words = (c[..., 0::2] | (c[..., 1::2] << 4)).reshape(k // 512, 128, 2 * n)
    return np.ascontiguousarray(words), np.ascontiguousarray(byte.astype(np.uint8).reshape(k // 512, 16, n))


def unpack_weight(words, scales, fmt):
    g, _, n = scales.shape
    words = np.ascontiguousarray(words).reshape(g, 128, n, -1)
    if fmt == "e4m3":
        vals = words.view(ml_dtypes.float8_e4m3fn).astype(np.float64)
    else:
        nib = np.empty((g, 128, n, 4), np.uint8)
        nib[..., 0::2] = words & 0xF
        nib[..., 1::2] = words >> 4
        vals = E2M1[nib]
    vals = vals * np.repeat(np.exp2(scales.astype(np.float64) - 127.0), 8, axis=1)[..., None]
    return vals.transpose(0, 1, 3, 2).reshape(g * 512, n)


B, N, T, D, DV, NQ = 1, 1024, 4096, 1024, 256, 128


def setup_inputs():
    n = np.random.standard_normal
    idx = np.sort(np.random.permutation(T)[:B * N].reshape(B, N), axis=1).reshape(-1)
    s = mx_kscale(D)[:, None]
    u = np.ones(T)
    u[idx] = mx_kscale(B * N)
    r = np.random.uniform(0.5, 2.0, T)
    qp = [pack_weight(x, "e4m3") for x in n((B, D, NQ)) * s * (0.80 / np.sqrt(D))]
    k = n((D, T)) / s
    v = n((DV, T)) / (u * r)
    kp = pack_weight(k, "e4m3")
    return {
        "q_words": np.stack([x[0] for x in qp]),
        "q_scales": np.stack([x[1] for x in qp]),
        "k_words": kp[0],
        "k_scales": kp[1],
        "vT": v.astype(np.float32),
        "vs": np.tile(u * r, (128, 1)).astype(np.float32),
        "kb": np.tile(n(T), (128, 1)).astype(np.float32),
        "og": n((B, NQ, DV)).astype(np.float32),
        "offs": striped(idx),
    }


def reference(q_words, q_scales, k_words, k_scales, vT, vs, kb, og, offs):
    idx = unstriped(offs)
    k = unpack_weight(k_words, k_scales, "e4m3")
    v = f64(vT)
    pick = lambda x: x[:, idx].reshape(x.shape[0], B, N).transpose(1, 0, 2)
    q = np.stack([unpack_weight(q_words[b], q_scales[b], "e4m3") for b in range(B)])
    score = q.transpose(0, 2, 1) @ pick(k)
    score = score + pick(f64(kb))[:, :1, :]
    p = np.square(np.maximum(score, 0.0))
    total = p.sum(-1, keepdims=True) + 1.0
    w = p * pick(f64(vs))[:, :1, :]
    y = mxq(w, 2, "e4m3") @ mxq(pick(v).transpose(0, 2, 1), 1, "e4m3")
    y = y / total
    y = y / (1.0 + np.exp(-f64(og)))
    return y

@@ -1,0 +1,185 @@
+from contextlib import ExitStack
+
+import concourse.mybir as mybir
+from concourse.masks import make_identity
+
+N, T, D, DV, NQ = 1024, 4096, 1024, 256, 128
+FLOPS = 2 * NQ * N * D + 2 * NQ * N * DV
+BYTES = D * T + D * T // 32 + 4 * DV * T + 2 * 4 * T + D * NQ + D * NQ // 32 + 2 * 4 * NQ * DV + 2 * 8 * N
+
+F32 = mybir.dt.float32
+BF16 = mybir.dt.bfloat16
+I32 = mybir.dt.int32
+U32 = mybir.dt.uint32
+U16 = mybir.dt.uint16
+U8 = mybir.dt.uint8
+X4 = mybir.dt.float8_e4m3fn_x4
+ACT = mybir.ActivationFunctionType
+ALU = mybir.AluOpType
+
+P = 128
+PASS = 512
+G = N // PASS
+O = D // PASS
+H = DV // P
+ROW = P - 1
+EARLY = T - (N - PASS)
+
+
+def tile_attend_rel2_kb_gate_srtq128n1024t4096_kernel(tc, q_words, q_scales, k_words, k_scales, vT, vs, kb, og, offs, out):
+    nc = tc.nc
+    with ExitStack() as ctx:
+        keep = ctx.enter_context(tc.tile_pool(name="keep", bufs=1))
+        psum = ctx.enter_context(tc.psum_pool(name="psum", bufs=1))
+
+        offsets = keep.tile([P, N // 16], U16, name="offsets")
+        nc.sync.dma_start(offsets[:], offs)
+
+        def slots(g):
+            return offsets[:, g * (PASS // 16):(g + 1) * (PASS // 16)]
+
+        kw = [keep.tile([P, T], I32, name="kw%d" % o) for o in range(O)]
+        vw = [keep.tile([P, T], F32, name="vw%d" % h) for h in range(H)]
+        ksw = keep.tile([P, T], U8, name="ksw")
+        kbw = keep.tile([P, T], F32, name="kbw")
+        vsw = keep.tile([P, T], F32, name="vsw")
+        qw = keep.tile([P, O, NQ], I32, name="qw", align_bytes=64)
+        qs = keep.tile([P, NQ], U8, name="qs", align_bytes=64)
+        ogt = keep.tile([P, DV], F32, name="ogt")
+        ident = keep.tile([P, P], F32, name="ident")
+
+        nc.vector.memset(ksw[:].bitcast(I32), 0)
+        nc.vector.memset(qs[:].bitcast(I32), 0)
+        nc.vector.memset(kbw[0:ROW, :], 0.0)
+        nc.vector.memset(vsw[0:ROW, :], 0.0)
+        make_identity(nc, ident[:])
+
+        def words(o):
+            return k_words[o].rearrange("g t r -> g (t r)").bitcast(I32)
+
+        nc.sync.dma_start(kw[0][:], words(0))
+        nc.scalar.dma_start(kbw[ROW:P, :], kb[0:1, :])
+        nc.scalar.dma_start(vsw[ROW:P, :], vs[0:1, :])
+        for q in range(4):
+            nc.scalar.dma_start(ksw[32 * q:32 * q + 8, :].bitcast(I32), k_scales[:, 4 * q:4 * q + 4, :].bitcast(I32))
+        nc.sync.dma_start(kw[1][:], words(1))
+        nc.sync.dma_start(qw[:], q_words[0].rearrange("o g q r -> g o (q r)").bitcast(I32))
+        nc.sync.dma_start(vw[0][:], vT[0:P, :])
+        nc.sync.dma_start(vw[1][:, 0:EARLY], vT[P:2 * P, 0:EARLY])
+        nc.sync.dma_start(vw[1][:, EARLY:T], vT[P:2 * P, EARLY:T])
+        for q in range(4):
+            nc.gpsimd.dma_start(qs[32 * q:32 * q + 8, :].bitcast(I32), q_scales[0][:, 4 * q:4 * q + 4, :].bitcast(I32))
+        nc.gpsimd.dma_start(ogt[:], og[0])
+
+        gate = keep.tile([P, DV], F32, name="gate")
+        nc.scalar.activation(gate[:], ogt[:], ACT.Sigmoid)
+
+        ksg = keep.tile([P, N], U8, name="ksg")
+        nc.vector.tensor_copy(ksg[:], ksw[:].indirect(offsets[:]))
+        ksp = keep.tile([P, G, 4, P], U8, name="ksp", align_bytes=64)
+        nc.vector.tensor_copy(ksp[:], ksg[:].rearrange("p (g s t) -> p g t s", g=G, t=4))
+
+        def token_columns(window, name):
+            picked = keep.tile([P, N], F32, name=name + "g")
+            nc.vector.tensor_copy(picked[:], window[:].indirect(offsets[:]))
+            cols = keep.tile([P, G, 4], F32, name=name + "c")
+            for g in range(G):
+                turned = psum.tile([P, 4, P], F32, name=name + "t%d" % g, tag="turn%d" % g)
+                for t in range(4):
+                    nc.tensor.transpose(turned[:, t, :], picked[:, g * PASS + t:(g + 1) * PASS:4], ident[:])
+                nc.scalar.copy(cols[:, g, :], turned[:, :, ROW])
+            return cols
+
+        kg = [keep.tile([P, G, 4, P], U32, name="kg%d" % o, align_bytes=64) for o in range(O)]
+
+        def gather_keys(o):
+            for g in range(G):
+                nc.vector.tensor_copy(kg[o][:, g].rearrange("p t s -> p s t"), kw[o][:].bitcast(U32).indirect(slots(g)))
+
+        kbc = token_columns(kbw, "kb")
+        gather_keys(0)
+        gather_keys(1)
+        vsc = token_columns(vsw, "vs")
+
+        rel = keep.tile([P, G, 4, NQ], F32, name="rel")
+        prob = keep.tile([P, G, NQ, 4], F32, name="prob")
+        for g in range(G):
+            score = psum.tile([P, 4, NQ], F32, name="score%d" % g)
+            for t in range(4):
+                for o in range(O):
+                    nc.tensor.matmul_mx(
+                        out=score[:, t, :],
+                        lhsT=kg[o][:, g, t, :].bitcast(X4), lhsT_scale=ksp[4 * o:P, g, t, :],
+                        rhs=qw[:, o, :].bitcast(X4), rhs_scale=qs[4 * o:P, :],
+                        start=(o == 0), stop=(o == O - 1))
+            for t in range(4):
+                nc.scalar.activation(rel[:, g, t, :], score[:, t, :], ACT.Relu, bias=kbc[:, g, t:t + 1])
+            nc.scalar.activation(prob[:, g], rel[:, g].rearrange("p t q -> p q t"), ACT.Square)
+
+        vb = [keep.tile([P, G, 2, P, 2], BF16, name="vb%d" % h) for h in range(H)]
+        vin = [[keep.tile([P, P, 4], BF16, name="vin%d%d" % (h, g), align_bytes=64) for g in range(G)] for h in range(H)]
+        vq = [[keep.tile([P, P], U32, name="vq%d%d" % (h, g), align_bytes=64) for g in range(G)] for h in range(H)]
+        vqs = [[keep.tile([P, P], U8, name="vqs%d%d" % (h, g), align_bytes=64) for g in range(G)] for h in range(H)]
+
+        def gather_values(h, g):
+            window = vw[h][:, 0:EARLY] if (h, g) == (H - 1, 0) else vw[h][:]
+            nc.vector.tensor_copy(vb[h][:, g].rearrange("p u s j -> p s u j"), window.indirect(slots(g)))
+            turned = psum.tile([P, 2, P], F32, name="vt%d%d" % (h, g), tag="vt%d" % g)
+            for u in range(2):
+                nc.tensor.transpose(turned[:, u, :], vb[h][:, g, u].rearrange("p s j -> p (s j)").bitcast(F32), ident[:])
+            nc.scalar.copy(vin[h][g][:].rearrange("p e t -> p (e t)").bitcast(F32).rearrange("p (e u) -> p e u", u=2),
+                           turned[:].rearrange("p u e -> p e u"))
+
+        def quantize_values(h, g):
+            nc.vector.quantize_mx(out=vq[h][g][:].bitcast(X4), scales=vqs[h][g][:],
+                                  in_=vin[h][g][:].rearrange("p e t -> p (e t)"))
+
+        wb = [keep.tile([P, NQ, 4], BF16, name="wb%d" % g, align_bytes=64) for g in range(G)]
+        wq = [keep.tile([P, NQ], U32, name="wq%d" % g, align_bytes=64) for g in range(G)]
+        wqs = [keep.tile([P, NQ], U8, name="wqs%d" % g, align_bytes=64) for g in range(G)]
+
+        def weigh(g):
+            nc.vector.tensor_tensor(wb[g][:], prob[:, g], vsc[:, g, :].unsqueeze(1).to_broadcast([P, NQ, 4]), ALU.mult)
+
+        def quantize_weights(g):
+            nc.vector.quantize_mx(out=wq[g][:].bitcast(X4), scales=wqs[g][:], in_=wb[g][:].rearrange("p q t -> p (q t)"))
+
+        weigh(0)
+        gather_values(0, 0)
+        gather_values(0, 1)
+        weigh(1)
+        quantize_weights(0)
+        quantize_values(0, 0)
+        quantize_weights(1)
+        quantize_values(0, 1)
+
+        part = keep.tile([P, G], F32, name="part")
+        squares = keep.tile([P, PASS], F32, name="squares")
+        for g in range(G):
+            back = psum.tile([P, 4, P], F32, name="back%d" % g, tag="turn%d" % g)
+            for t in range(4):
+                nc.tensor.transpose(back[:, t, :], rel[:, g, t, :], ident[:])
+            nc.scalar.activation(squares[:], back[:].rearrange("p t s -> p (t s)"), ACT.Square, accum_out=part[:, g:g + 1])
+        total = keep.tile([P, 1], F32, name="total")
+        nc.vector.tensor_scalar(total[:], part[:, 0:1], part[:, 1:2], 1.0, ALU.add, ALU.add)
+        inv = keep.tile([P, 1], F32, name="inv")
+        nc.vector.reciprocal(inv[:], total[:])
+        factor = keep.tile([P, DV], F32, name="factor")
+        nc.scalar.activation(factor[:], gate[:], ACT.Copy, scale=inv[:])
+
+        def finish(h):
+            y = psum.tile([P, P], F32, name="y%d" % h)
+            for g in range(G):
+                nc.tensor.matmul_mx(out=y[:], lhsT=wq[g][:].bitcast(X4), lhsT_scale=wqs[g][:],
+                                    rhs=vq[h][g][:].bitcast(X4), rhs_scale=vqs[h][g][:],
+                                    start=(g == 0), stop=(g == G - 1))
+            res = keep.tile([P, P], F32, name="res%d" % h)
+            nc.vector.tensor_tensor(res[:], y[:], factor[:, h * P:(h + 1) * P], ALU.mult)
+            nc.sync.dma_start(out[0][:, h * P:(h + 1) * P], res[:])
+
+        finish(0)
+        gather_values(1, 0)
+        gather_values(1, 1)
+        quantize_values(1, 0)
+        quantize_values(1, 1)
+        finish(1)

@@ -38,68 +38,88 @@ def tile_attend_rel2_kb_gate_srtq128n1024t4096_kernel(tc, q_words, q_scales, k_w
         def slots(g):
             return offsets[:, g * (PASS // 16):(g + 1) * (PASS // 16)]
 
-        kw = [keep.tile([P, T], I32, name="kw%d" % o) for o in range(O)]
-        vw = [keep.tile([P, T], F32, name="vw%d" % h) for h in range(H)]
+        kbw = keep.tile([P, T], F32, name="kbw", tag="first")
+        kw = [keep.tile([P, T], I32, name="kw0", tag="second"), keep.tile([P, T], I32, name="kw1")]
         ksw = keep.tile([P, T], U8, name="ksw")
-        kbw = keep.tile([P, T], F32, name="kbw")
         vsw = keep.tile([P, T], F32, name="vsw")
         qw = keep.tile([P, O, NQ], I32, name="qw", align_bytes=64)
         qs = keep.tile([P, NQ], U8, name="qs", align_bytes=64)
         ogt = keep.tile([P, DV], F32, name="ogt")
         ident = keep.tile([P, P], F32, name="ident")
 
+        identb = keep.tile([P, P], BF16, name="identb")
         nc.vector.memset(ksw[:].bitcast(I32), 0)
-        nc.vector.memset(qs[:].bitcast(I32), 0)
         nc.vector.memset(kbw[0:ROW, :], 0.0)
-        nc.vector.memset(vsw[0:ROW, :], 0.0)
+        nc.gpsimd.memset(qs[:].bitcast(I32), 0)
         make_identity(nc, ident[:])
+        make_identity(nc, identb[:])
+        for c in range(0, T, 1024):
+            nc.gpsimd.memset(vsw[0:ROW, c:c + 1024], 0.0)
+
+        def by_block(ap):
+            return ap.rearrange("p t (b r) -> p b t r", r=8)
 
         def words(o):
             return k_words[o].rearrange("g t r -> g (t r)").bitcast(I32)
 
-        nc.sync.dma_start(kw[0][:], words(0))
-        nc.scalar.dma_start(kbw[ROW:P, :], kb[0:1, :])
-        nc.scalar.dma_start(vsw[ROW:P, :], vs[0:1, :])
-        for q in range(4):
-            nc.scalar.dma_start(ksw[32 * q:32 * q + 8, :].bitcast(I32), k_scales[:, 4 * q:4 * q + 4, :].bitcast(I32))
-        nc.sync.dma_start(kw[1][:], words(1))
+        nc.sync.dma_start(kbw[ROW:P, :], kb[0:1, :])
+        nc.sync.dma_start(vsw[ROW:P, :], vs[0:1, :])
         nc.sync.dma_start(qw[:], q_words[0].rearrange("o g q r -> g o (q r)").bitcast(I32))
-        nc.sync.dma_start(vw[0][:], vT[0:P, :])
-        nc.sync.dma_start(vw[1][:, 0:EARLY], vT[P:2 * P, 0:EARLY])
-        nc.sync.dma_start(vw[1][:, EARLY:T], vT[P:2 * P, EARLY:T])
+        nc.sync.dma_start(ogt[:], og[0])
+        nc.sync.dma_start(kw[0][:], words(0))
+        nc.sync.dma_start(kw[1][:], words(1))
+        for q in range(2):
+            nc.scalar.dma_start(ksw[32 * q:32 * q + 8, :].bitcast(I32), k_scales[:, 4 * q:4 * q + 4, :].bitcast(I32))
+        for q in range(2, 4):
+            for o in range(O):
+                nc.scalar.dma_start(ksw[32 * q + 4 * o:32 * q + 4 * o + 4, :].bitcast(I32),
+                                    k_scales[o, 4 * q:4 * q + 4, :].bitcast(I32))
         for q in range(4):
             nc.gpsimd.dma_start(qs[32 * q:32 * q + 8, :].bitcast(I32), q_scales[0][:, 4 * q:4 * q + 4, :].bitcast(I32))
-        nc.gpsimd.dma_start(ogt[:], og[0])
 
         gate = keep.tile([P, DV], F32, name="gate")
         nc.scalar.activation(gate[:], ogt[:], ACT.Sigmoid)
 
         ksg = keep.tile([P, N], U8, name="ksg")
-        nc.vector.tensor_copy(ksg[:], ksw[:].indirect(offsets[:]))
         ksp = keep.tile([P, G, 4, P], U8, name="ksp", align_bytes=64)
-        nc.vector.tensor_copy(ksp[:], ksg[:].rearrange("p (g s t) -> p g t s", g=G, t=4))
+
+        def gather_scales():
+            nc.vector.tensor_copy(ksg[:], ksw[:].indirect(offsets[:]))
+            nc.vector.tensor_copy(
+                ksp[:].rearrange("p g t s -> p (g t s)").bitcast(I32).rearrange("p (g t b w) -> p g t b w", g=G, t=4, w=2),
+                ksg[:].bitcast(I32).rearrange("p (g b t w) -> p g t b w", g=G, t=4, w=2))
 
         def token_columns(window, name):
             picked = keep.tile([P, N], F32, name=name + "g")
             nc.vector.tensor_copy(picked[:], window[:].indirect(offsets[:]))
+            laid = keep.tile([P, G, 4, P], F32, name=name + "l")
+            for g in range(G):
+                nc.scalar.copy(laid[:, g].rearrange("p t (b r) -> p t b r", r=8),
+                               picked[:, g * PASS:(g + 1) * PASS].rearrange("p (b t r) -> p t b r", t=4, r=8))
             cols = keep.tile([P, G, 4], F32, name=name + "c")
             for g in range(G):
                 turned = psum.tile([P, 4, P], F32, name=name + "t%d" % g, tag="turn%d" % g)
                 for t in range(4):
-                    nc.tensor.transpose(turned[:, t, :], picked[:, g * PASS + t:(g + 1) * PASS:4], ident[:])
+                    nc.tensor.transpose(turned[:, t, :], laid[:, g, t, :], ident[:])
                 nc.scalar.copy(cols[:, g, :], turned[:, :, ROW])
             return cols
 
-        kg = [keep.tile([P, G, 4, P], U32, name="kg%d" % o, align_bytes=64) for o in range(O)]
+        kg = [[keep.tile([P, 4, P], U32, name="kg%d%d" % (o, g), tag="kg%d%d" % (o, g), align_bytes=64) for g in range(G)] for o in range(O)]
 
         def gather_keys(o):
             for g in range(G):
-                nc.vector.tensor_copy(kg[o][:, g].rearrange("p t s -> p s t"), kw[o][:].bitcast(U32).indirect(slots(g)))
+                nc.vector.tensor_copy(by_block(kg[o][g][:]), kw[o][:].bitcast(U32).indirect(slots(g)))
 
         kbc = token_columns(kbw, "kb")
+        vw = [keep.tile([P, T], F32, name="vw0", tag="first")]
+        nc.sync.dma_start(vw[0][:], vT[0:P, :])
         gather_keys(0)
-        gather_keys(1)
+        vw.append(keep.tile([P, T], F32, name="vw1", tag="second"))
+        nc.sync.dma_start(vw[1][:, 0:EARLY], vT[P:2 * P, 0:EARLY])
+        nc.sync.dma_start(vw[1][:, EARLY:T], vT[P:2 * P, EARLY:T])
         vsc = token_columns(vsw, "vs")
+        gather_scales()
+        gather_keys(1)
 
         rel = keep.tile([P, G, 4, NQ], F32, name="rel")
         prob = keep.tile([P, G, NQ, 4], F32, name="prob")
@@ -109,32 +129,32 @@ def tile_attend_rel2_kb_gate_srtq128n1024t4096_kernel(tc, q_words, q_scales, k_w
                 for o in range(O):
                     nc.tensor.matmul_mx(
                         out=score[:, t, :],
-                        lhsT=kg[o][:, g, t, :].bitcast(X4), lhsT_scale=ksp[4 * o:P, g, t, :],
+                        lhsT=kg[o][g][:, t, :].bitcast(X4), lhsT_scale=ksp[4 * o:P, g, t, :],
                         rhs=qw[:, o, :].bitcast(X4), rhs_scale=qs[4 * o:P, :],
                         start=(o == 0), stop=(o == O - 1))
             for t in range(4):
                 nc.scalar.activation(rel[:, g, t, :], score[:, t, :], ACT.Relu, bias=kbc[:, g, t:t + 1])
             nc.scalar.activation(prob[:, g], rel[:, g].rearrange("p t q -> p q t"), ACT.Square)
 
-        vb = [keep.tile([P, G, 2, P, 2], BF16, name="vb%d" % h) for h in range(H)]
-        vin = [[keep.tile([P, P, 4], BF16, name="vin%d%d" % (h, g), align_bytes=64) for g in range(G)] for h in range(H)]
+        vin = [[keep.tile([P, P, 4], BF16, name="vin%d%d" % (h, g), tag="vin%d%d" % (h, g), align_bytes=64) for g in range(G)] for h in range(H)]
         vq = [[keep.tile([P, P], U32, name="vq%d%d" % (h, g), align_bytes=64) for g in range(G)] for h in range(H)]
         vqs = [[keep.tile([P, P], U8, name="vqs%d%d" % (h, g), align_bytes=64) for g in range(G)] for h in range(H)]
 
         def gather_values(h, g):
             window = vw[h][:, 0:EARLY] if (h, g) == (H - 1, 0) else vw[h][:]
-            nc.vector.tensor_copy(vb[h][:, g].rearrange("p u s j -> p s u j"), window.indirect(slots(g)))
-            turned = psum.tile([P, 2, P], F32, name="vt%d%d" % (h, g), tag="vt%d" % g)
-            for u in range(2):
-                nc.tensor.transpose(turned[:, u, :], vb[h][:, g, u].rearrange("p s j -> p (s j)").bitcast(F32), ident[:])
-            nc.scalar.copy(vin[h][g][:].rearrange("p e t -> p (e t)").bitcast(F32).rearrange("p (e u) -> p e u", u=2),
-                           turned[:].rearrange("p u e -> p e u"))
+            slot = {(0, 0): "kg10", (0, 1): "kg11", (1, 0): "wb1", (1, 1): "vin01"}[(h, g)]
+            vb = keep.tile([P, 4, P], BF16, name="vb%d%d" % (h, g), tag=slot, align_bytes=64)
+            nc.vector.tensor_copy(by_block(vb[:]), window.indirect(slots(g)))
+            turned = psum.tile([P, 4, P], BF16, name="vt%d%d" % (h, g), tag="vt%d" % g)
+            for t in range(4):
+                nc.tensor.transpose(turned[:, t, :], vb[:, t, :], identb[:])
+            nc.scalar.copy(vin[h][g][:], turned[:].rearrange("p t e -> p e t"))
 
         def quantize_values(h, g):
             nc.vector.quantize_mx(out=vq[h][g][:].bitcast(X4), scales=vqs[h][g][:],
                                   in_=vin[h][g][:].rearrange("p e t -> p (e t)"))
 
-        wb = [keep.tile([P, NQ, 4], BF16, name="wb%d" % g, align_bytes=64) for g in range(G)]
+        wb = [keep.tile([P, NQ, 4], BF16, name="wb%d" % g, tag="wb%d" % g, align_bytes=64) for g in range(G)]
         wq = [keep.tile([P, NQ], U32, name="wq%d" % g, align_bytes=64) for g in range(G)]
         wqs = [keep.tile([P, NQ], U8, name="wqs%d" % g, align_bytes=64) for g in range(G)]
 

@@ -23,6 +23,7 @@ G = N // PASS
 O = D // PASS
 H = DV // P
 ROW = P - 1
+ZEROED = 2816
 EARLY = T - (N - PASS)
 
 
@@ -38,23 +39,22 @@ def tile_attend_rel2_kb_gate_srtq128n1024t4096_kernel(tc, q_words, q_scales, k_w
         def slots(g):
             return offsets[:, g * (PASS // 16):(g + 1) * (PASS // 16)]
 
-        kbw = keep.tile([P, T], F32, name="kbw", tag="first")
-        kw = [keep.tile([P, T], I32, name="kw0", tag="second"), keep.tile([P, T], I32, name="kw1")]
-        ksw = keep.tile([P, T], U8, name="ksw")
-        vsw = keep.tile([P, T], F32, name="vsw")
+        kbw = keep.tile([P, T], F32, name="kbw", tag="bias", align_bytes=64)
+        vsw = keep.tile([P, T], F32, name="vsw", tag="scale", align_bytes=64)
+        ksw = keep.tile([P, T], U8, name="ksw", tag="bytes", align_bytes=64)
+        ogt = keep.tile([P, DV], F32, name="ogt", tag="logits", align_bytes=64)
+        kw = [keep.tile([P, T], I32, name="kw0", tag="keys", align_bytes=64)]
         qw = keep.tile([P, O, NQ], I32, name="qw", align_bytes=64)
         qs = keep.tile([P, NQ], U8, name="qs", align_bytes=64)
-        ogt = keep.tile([P, DV], F32, name="ogt")
+        kbs = keep.tile([P, 32], F32, name="kbs")
+        vss = keep.tile([P, 32], F32, name="vss")
         ident = keep.tile([P, P], F32, name="ident")
-
         identb = keep.tile([P, P], BF16, name="identb")
-        nc.vector.memset(ksw[:].bitcast(I32), 0)
-        nc.vector.memset(kbw[0:ROW, :], 0.0)
-        nc.gpsimd.memset(qs[:].bitcast(I32), 0)
         make_identity(nc, ident[:])
         make_identity(nc, identb[:])
-        for c in range(0, T, 1024):
-            nc.gpsimd.memset(vsw[0:ROW, c:c + 1024], 0.0)
+        nc.vector.memset(ksw[:].bitcast(I32), 0)
+        nc.vector.memset(kbw[0:ROW, 0:ZEROED], 0.0)
+        nc.vector.memset(qs[:].bitcast(I32), 0)
 
         def by_block(ap):
             return ap.rearrange("p t (b r) -> p b t r", r=8)
@@ -62,23 +62,28 @@ def tile_attend_rel2_kb_gate_srtq128n1024t4096_kernel(tc, q_words, q_scales, k_w
         def words(o):
             return k_words[o].rearrange("g t r -> g (t r)").bitcast(I32)
 
+        nc.sync.dma_start(ogt[:], og[0])
+        nc.sync.dma_start(kbs[:], kb[:, 0:32])
         nc.sync.dma_start(kbw[ROW:P, :], kb[0:1, :])
+        nc.sync.dma_start(vss[:], vs[:, 0:32])
         nc.sync.dma_start(vsw[ROW:P, :], vs[0:1, :])
         nc.sync.dma_start(qw[:], q_words[0].rearrange("o g q r -> g o (q r)").bitcast(I32))
-        nc.sync.dma_start(ogt[:], og[0])
         nc.sync.dma_start(kw[0][:], words(0))
-        nc.sync.dma_start(kw[1][:], words(1))
         for q in range(2):
-            nc.scalar.dma_start(ksw[32 * q:32 * q + 8, :].bitcast(I32), k_scales[:, 4 * q:4 * q + 4, :].bitcast(I32))
+            nc.sync.dma_start(ksw[32 * q:32 * q + 8, :].bitcast(I32), k_scales[:, 4 * q:4 * q + 4, :].bitcast(I32))
         for q in range(2, 4):
             for o in range(O):
-                nc.scalar.dma_start(ksw[32 * q + 4 * o:32 * q + 4 * o + 4, :].bitcast(I32),
-                                    k_scales[o, 4 * q:4 * q + 4, :].bitcast(I32))
-        for q in range(4):
-            nc.gpsimd.dma_start(qs[32 * q:32 * q + 8, :].bitcast(I32), q_scales[0][:, 4 * q:4 * q + 4, :].bitcast(I32))
-
+                nc.sync.dma_start(ksw[32 * q + 4 * o:32 * q + 4 * o + 4, :].bitcast(I32),
+                                  k_scales[o, 4 * q:4 * q + 4, :].bitcast(I32))
         gate = keep.tile([P, DV], F32, name="gate")
         nc.scalar.activation(gate[:], ogt[:], ACT.Sigmoid)
+        kw.append(keep.tile([P, T], I32, name="kw1", tag="logits", align_bytes=64))
+        nc.sync.dma_start(kw[1][:], words(1))
+        for q in range(4):
+            nc.sync.dma_start(qs[32 * q:32 * q + 8, :].bitcast(I32), q_scales[0][:, 4 * q:4 * q + 4, :].bitcast(I32))
+        for window, source, first in ((kbw, kbs, ZEROED), (vsw, vss, 0)):
+            nc.scalar.activation(window[0:ROW, first:T].rearrange("p (a b) -> p a b", b=32),
+                                 source[0:ROW, :].unsqueeze(1).to_broadcast([ROW, (T - first) // 32, 32]), ACT.Copy)
 
         ksg = keep.tile([P, N], U8, name="ksg")
         ksp = keep.tile([P, G, 4, P], U8, name="ksp", align_bytes=64)
@@ -89,40 +94,38 @@ def tile_attend_rel2_kb_gate_srtq128n1024t4096_kernel(tc, q_words, q_scales, k_w
                 ksp[:].rearrange("p g t s -> p (g t s)").bitcast(I32).rearrange("p (g t b w) -> p g t b w", g=G, t=4, w=2),
                 ksg[:].bitcast(I32).rearrange("p (g b t w) -> p g t b w", g=G, t=4, w=2))
 
-        def token_columns(window, name):
-            picked = keep.tile([P, N], F32, name=name + "g")
-            nc.vector.tensor_copy(picked[:], window[:].indirect(offsets[:]))
-            laid = keep.tile([P, G, 4, P], F32, name=name + "l")
+        def token_columns(window, name, tag):
+            laid = keep.tile([P, G, 4, P], U32, name=name + "g", tag=tag, align_bytes=64)
             for g in range(G):
-                nc.scalar.copy(laid[:, g].rearrange("p t (b r) -> p t b r", r=8),
-                               picked[:, g * PASS:(g + 1) * PASS].rearrange("p (b t r) -> p t b r", t=4, r=8))
+                nc.vector.tensor_copy(by_block(laid[:, g]), window[:].bitcast(U32).indirect(slots(g)))
             cols = keep.tile([P, G, 4], F32, name=name + "c")
             for g in range(G):
                 turned = psum.tile([P, 4, P], F32, name=name + "t%d" % g, tag="turn%d" % g)
                 for t in range(4):
-                    nc.tensor.transpose(turned[:, t, :], laid[:, g, t, :], ident[:])
+                    nc.tensor.transpose(turned[:, t, :], laid[:, g, t, :].bitcast(F32), ident[:])
                 nc.scalar.copy(cols[:, g, :], turned[:, :, ROW])
             return cols
 
-        kg = [[keep.tile([P, 4, P], U32, name="kg%d%d" % (o, g), tag="kg%d%d" % (o, g), align_bytes=64) for g in range(G)] for o in range(O)]
+        kg = []
 
-        def gather_keys(o):
+        def gather_keys(o, tags):
+            kg.append([keep.tile([P, 4, P], U32, name="kg%d%d" % (o, g), tag=tags[g], align_bytes=64) for g in range(G)])
             for g in range(G):
                 nc.vector.tensor_copy(by_block(kg[o][g][:]), kw[o][:].bitcast(U32).indirect(slots(g)))
 
-        kbc = token_columns(kbw, "kb")
-        vw = [keep.tile([P, T], F32, name="vw0", tag="first")]
+        kbc = token_columns(kbw, "kb", "kbg")
+        vw = [keep.tile([P, T], F32, name="vw0", tag="bias", align_bytes=64)]
         nc.sync.dma_start(vw[0][:], vT[0:P, :])
-        gather_keys(0)
-        vw.append(keep.tile([P, T], F32, name="vw1", tag="second"))
+        gather_keys(0, ("kg00", "kg01"))
+        vsc = token_columns(vsw, "vs", "keys")
+        vw.append(keep.tile([P, T], F32, name="vw1", tag="scale", align_bytes=64))
         nc.sync.dma_start(vw[1][:, 0:EARLY], vT[P:2 * P, 0:EARLY])
         nc.sync.dma_start(vw[1][:, EARLY:T], vT[P:2 * P, EARLY:T])
-        vsc = token_columns(vsw, "vs")
         gather_scales()
-        gather_keys(1)
+        gather_keys(1, ("bytes", "kg11"))
 
         rel = keep.tile([P, G, 4, NQ], F32, name="rel")
-        prob = keep.tile([P, G, NQ, 4], F32, name="prob")
+        prob = keep.tile([P, G, 4, NQ], F32, name="prob")
         for g in range(G):
             score = psum.tile([P, 4, NQ], F32, name="score%d" % g)
             for t in range(4):
@@ -134,7 +137,7 @@ def tile_attend_rel2_kb_gate_srtq128n1024t4096_kernel(tc, q_words, q_scales, k_w
                         start=(o == 0), stop=(o == O - 1))
             for t in range(4):
                 nc.scalar.activation(rel[:, g, t, :], score[:, t, :], ACT.Relu, bias=kbc[:, g, t:t + 1])
-            nc.scalar.activation(prob[:, g], rel[:, g].rearrange("p t q -> p q t"), ACT.Square)
+            nc.scalar.activation(prob[:, g], rel[:, g], ACT.Square)
 
         vin = [[keep.tile([P, P, 4], BF16, name="vin%d%d" % (h, g), tag="vin%d%d" % (h, g), align_bytes=64) for g in range(G)] for h in range(H)]
         vq = [[keep.tile([P, P], U32, name="vq%d%d" % (h, g), align_bytes=64) for g in range(G)] for h in range(H)]
@@ -142,8 +145,7 @@ def tile_attend_rel2_kb_gate_srtq128n1024t4096_kernel(tc, q_words, q_scales, k_w
 
         def gather_values(h, g):
             window = vw[h][:, 0:EARLY] if (h, g) == (H - 1, 0) else vw[h][:]
-            slot = {(0, 0): "kg10", (0, 1): "kg11", (1, 0): "wb1", (1, 1): "vin01"}[(h, g)]
-            vb = keep.tile([P, 4, P], BF16, name="vb%d%d" % (h, g), tag=slot, align_bytes=64)
+            vb = keep.tile([P, 4, P], BF16, name="vb%d%d" % (h, g), align_bytes=64)
             nc.vector.tensor_copy(by_block(vb[:]), window.indirect(slots(g)))
             turned = psum.tile([P, 4, P], BF16, name="vt%d%d" % (h, g), tag="vt%d" % g)
             for t in range(4):
@@ -154,35 +156,37 @@ def tile_attend_rel2_kb_gate_srtq128n1024t4096_kernel(tc, q_words, q_scales, k_w
             nc.vector.quantize_mx(out=vq[h][g][:].bitcast(X4), scales=vqs[h][g][:],
                                   in_=vin[h][g][:].rearrange("p e t -> p (e t)"))
 
-        wb = [keep.tile([P, NQ, 4], BF16, name="wb%d" % g, tag="wb%d" % g, align_bytes=64) for g in range(G)]
         wq = [keep.tile([P, NQ], U32, name="wq%d" % g, align_bytes=64) for g in range(G)]
         wqs = [keep.tile([P, NQ], U8, name="wqs%d" % g, align_bytes=64) for g in range(G)]
 
         def weigh(g):
-            nc.vector.tensor_tensor(wb[g][:], prob[:, g], vsc[:, g, :].unsqueeze(1).to_broadcast([P, NQ, 4]), ALU.mult)
+            nc.vector.tensor_tensor(wb[:, g], prob[:, g].rearrange("p t q -> p q t"), vsc[:, g, :].unsqueeze(1).to_broadcast([P, NQ, 4]), ALU.mult)
 
         def quantize_weights(g):
-            nc.vector.quantize_mx(out=wq[g][:].bitcast(X4), scales=wqs[g][:], in_=wb[g][:].rearrange("p q t -> p (q t)"))
+            nc.vector.quantize_mx(out=wq[g][:].bitcast(X4), scales=wqs[g][:], in_=wb[:, g].rearrange("p q t -> p (q t)"))
 
-        weigh(0)
         gather_values(0, 0)
         gather_values(0, 1)
+        wb = keep.tile([P, G, NQ, 4], BF16, name="wb", tag="bias", align_bytes=64)
+        weigh(0)
         weigh(1)
         quantize_weights(0)
         quantize_values(0, 0)
         quantize_weights(1)
         quantize_values(0, 1)
 
-        part = keep.tile([P, G], F32, name="part")
-        squares = keep.tile([P, PASS], F32, name="squares")
-        for g in range(G):
-            back = psum.tile([P, 4, P], F32, name="back%d" % g, tag="turn%d" % g)
-            for t in range(4):
-                nc.tensor.transpose(back[:, t, :], rel[:, g, t, :], ident[:])
-            nc.scalar.activation(squares[:], back[:].rearrange("p t s -> p (t s)"), ACT.Square, accum_out=part[:, g:g + 1])
+        back = psum.tile([P, P], F32, name="back", tag="vt1")
+        for i in range(4 * G):
+            nc.tensor.matmul(back[:], prob[:, i // 4, i % 4, :], ident[:], start=(i == 0), stop=(i == 4 * G - 1), is_transpose=True)
+        spare = keep.tile([P, P], F32, name="spare")
         total = keep.tile([P, 1], F32, name="total")
-        nc.vector.tensor_scalar(total[:], part[:, 0:1], part[:, 1:2], 1.0, ALU.add, ALU.add)
-        inv = keep.tile([P, 1], F32, name="inv")
+        nc.scalar.activation(spare[:], back[:], ACT.Copy, bias=1.0 / P, accum_out=total[:])
+        gather_values(1, 0)
+        gather_values(1, 1)
+        quantize_values(1, 0)
+        quantize_values(1, 1)
+
+        inv = keep.tile([P, 1], F32, name="inv", tag="scale", align_bytes=64)
         nc.vector.reciprocal(inv[:], total[:])
         factor = keep.tile([P, DV], F32, name="factor")
         nc.scalar.activation(factor[:], gate[:], ACT.Copy, scale=inv[:])
@@ -198,8 +202,4 @@ def tile_attend_rel2_kb_gate_srtq128n1024t4096_kernel(tc, q_words, q_scales, k_w
             nc.sync.dma_start(out[0][:, h * P:(h + 1) * P], res[:])
 
         finish(0)
-        gather_values(1, 0)
-        gather_values(1, 1)
-        quantize_values(1, 0)
-        quantize_values(1, 1)
         finish(1)

@@ -23,8 +23,8 @@ G = N // PASS
 O = D // PASS
 H = DV // P
 ROW = P - 1
-ZEROED = 2816
 EARLY = T - (N - PASS)
+RAW = 96
 
 
 def tile_attend_rel2_kb_gate_srtq128n1024t4096_kernel(tc, q_words, q_scales, k_words, k_scales, vT, vs, kb, og, offs, out):
@@ -39,114 +39,108 @@ def tile_attend_rel2_kb_gate_srtq128n1024t4096_kernel(tc, q_words, q_scales, k_w
         def slots(g):
             return offsets[:, g * (PASS // 16):(g + 1) * (PASS // 16)]
 
-        kbw = keep.tile([P, T], F32, name="kbw", tag="bias", align_bytes=64)
-        vsw = keep.tile([P, T], F32, name="vsw", tag="scale", align_bytes=64)
-        ksw = keep.tile([P, T], U8, name="ksw", tag="bytes", align_bytes=64)
-        ogt = keep.tile([P, DV], F32, name="ogt", tag="logits", align_bytes=64)
-        kw = [keep.tile([P, T], I32, name="kw0", tag="keys", align_bytes=64)]
-        qw = keep.tile([P, O, NQ], I32, name="qw", align_bytes=64)
-        qs = keep.tile([P, NQ], U8, name="qs", align_bytes=64)
-        kbs = keep.tile([P, 32], F32, name="kbs")
-        vss = keep.tile([P, 32], F32, name="vss")
-        ident = keep.tile([P, P], F32, name="ident")
-        identb = keep.tile([P, P], BF16, name="identb")
-        make_identity(nc, ident[:])
-        make_identity(nc, identb[:])
-        nc.vector.memset(ksw[:].bitcast(I32), 0)
-        nc.vector.memset(kbw[0:ROW, 0:ZEROED], 0.0)
-        nc.vector.memset(qs[:].bitcast(I32), 0)
-
         def by_block(ap):
             return ap.rearrange("p t (b r) -> p b t r", r=8)
 
         def words(o):
             return k_words[o].rearrange("g t r -> g (t r)").bitcast(I32)
 
-        nc.sync.dma_start(ogt[:], og[0])
-        nc.sync.dma_start(kbs[:], kb[:, 0:32])
+        def load_window(tile, source):
+            nc.sync.dma_start(tile[:, 0:EARLY], source[:, 0:EARLY])
+            nc.sync.dma_start(tile[:, EARLY:T], source[:, EARLY:T])
+
+        def window(tile, g):
+            return tile[:, 0:EARLY] if g == 0 else tile[:]
+
+        kbw = keep.tile([P, T], F32, name="kbw", tag="bias", align_bytes=64)
+        vsw = keep.tile([P, T], F32, name="vsw", align_bytes=64)
+        ksw = keep.tile([P, T], U8, name="ksw", align_bytes=64)
+        ogt = keep.tile([P, DV], F32, name="ogt", align_bytes=64)
+        kw = [keep.tile([P, T], I32, name="kw0", tag="keys", align_bytes=64)]
+        qw = keep.tile([P, O, NQ], I32, name="qw", align_bytes=64)
+        ksr = keep.tile([P, N + NQ], U8, name="ksr", align_bytes=64)
+        vss = keep.tile([P, 32], F32, name="vss")
+        ksp = keep.tile([P, O, N + NQ], U8, name="ksp", align_bytes=64)
+        ident = keep.tile([P, P], F32, name="ident")
+        identb = keep.tile([P, P], BF16, name="identb")
+
+        nc.sync.dma_start(ksw[RAW:P, :].bitcast(I32), k_scales.rearrange("o f t -> f o t").bitcast(I32))
         nc.sync.dma_start(kbw[ROW:P, :], kb[0:1, :])
+        nc.sync.dma_start(ogt[:], og[0])
         nc.sync.dma_start(vss[:], vs[:, 0:32])
         nc.sync.dma_start(vsw[ROW:P, :], vs[0:1, :])
-        nc.sync.dma_start(qw[:], q_words[0].rearrange("o g q r -> g o (q r)").bitcast(I32))
+        nc.sync.dma_start(ksr[RAW:P, N:N + NQ].bitcast(I32), q_scales[0].rearrange("o f q -> f o q").bitcast(I32))
         nc.sync.dma_start(kw[0][:], words(0))
-        for q in range(2):
-            nc.sync.dma_start(ksw[32 * q:32 * q + 8, :].bitcast(I32), k_scales[:, 4 * q:4 * q + 4, :].bitcast(I32))
-        for q in range(2, 4):
-            for o in range(O):
-                nc.sync.dma_start(ksw[32 * q + 4 * o:32 * q + 4 * o + 4, :].bitcast(I32),
-                                  k_scales[o, 4 * q:4 * q + 4, :].bitcast(I32))
+        nc.sync.dma_start(qw[:], q_words[0].rearrange("o g q r -> g o (q r)").bitcast(I32))
+
+        nc.gpsimd.memset(ksw[0:RAW, :].bitcast(I32), 0)
+        nc.gpsimd.memset(kbw[0:ROW, :], 0.0)
+        nc.vector.memset(ksp[:].rearrange("p o n -> p (o n)").bitcast(I32), 0)
+        make_identity(nc, ident[:])
+        make_identity(nc, identb[:])
+
         gate = keep.tile([P, DV], F32, name="gate")
         nc.scalar.activation(gate[:], ogt[:], ACT.Sigmoid)
-        kw.append(keep.tile([P, T], I32, name="kw1", tag="logits", align_bytes=64))
-        nc.sync.dma_start(kw[1][:], words(1))
+        nc.scalar.activation(vsw[0:ROW, :].rearrange("p (a b) -> p a b", b=32),
+                             vss[0:ROW, :].unsqueeze(1).to_broadcast([ROW, T // 32, 32]), ACT.Copy)
+
+        ksg = keep.tile([P, N], U8, name="ksg", tag="logits", align_bytes=64)
+        nc.vector.tensor_copy(ksg[:], ksw[:].indirect(offsets[:]))
+        nc.vector.tensor_copy(
+            ksr[RAW:P, 0:N].bitcast(I32).rearrange("p (g t b w) -> p g t b w", g=G, t=4, w=2),
+            ksg[RAW:P, :].bitcast(I32).rearrange("p (g b t w) -> p g t b w", g=G, t=4, w=2))
         for q in range(4):
-            nc.sync.dma_start(qs[32 * q:32 * q + 8, :].bitcast(I32), q_scales[0][:, 4 * q:4 * q + 4, :].bitcast(I32))
-        for window, source, first in ((kbw, kbs, ZEROED), (vsw, vss, 0)):
-            nc.scalar.activation(window[0:ROW, first:T].rearrange("p (a b) -> p a b", b=32),
-                                 source[0:ROW, :].unsqueeze(1).to_broadcast([ROW, (T - first) // 32, 32]), ACT.Copy)
+            nc.sync.dma_start(ksp[32 * q:32 * q + 4].bitcast(I32), ksr[RAW + 8 * q:RAW + 8 * q + 8, :].bitcast(I32))
+        kw.append(keep.tile([P, T], I32, name="kw1", tag="logits", align_bytes=64))
+        load_window(kw[1], words(1))
 
-        ksg = keep.tile([P, N], U8, name="ksg")
-        ksp = keep.tile([P, G, 4, P], U8, name="ksp", align_bytes=64)
-
-        def gather_scales():
-            nc.vector.tensor_copy(ksg[:], ksw[:].indirect(offsets[:]))
-            nc.vector.tensor_copy(
-                ksp[:].rearrange("p g t s -> p (g t s)").bitcast(I32).rearrange("p (g t b w) -> p g t b w", g=G, t=4, w=2),
-                ksg[:].bitcast(I32).rearrange("p (g b t w) -> p g t b w", g=G, t=4, w=2))
-
-        def token_columns(window, name, tag):
-            laid = keep.tile([P, G, 4, P], U32, name=name + "g", tag=tag, align_bytes=64)
-            for g in range(G):
-                nc.vector.tensor_copy(by_block(laid[:, g]), window[:].bitcast(U32).indirect(slots(g)))
-            cols = keep.tile([P, G, 4], F32, name=name + "c")
-            for g in range(G):
-                turned = psum.tile([P, 4, P], F32, name=name + "t%d" % g, tag="turn%d" % g)
-                for t in range(4):
-                    nc.tensor.transpose(turned[:, t, :], laid[:, g, t, :].bitcast(F32), ident[:])
-                nc.scalar.copy(cols[:, g, :], turned[:, :, ROW])
+        def token_column(source, name, g, tag):
+            laid = keep.tile([P, 4, P], U32, name=name + "g%d" % g, tag=tag, align_bytes=64)
+            nc.vector.tensor_copy(by_block(laid[:]), source[:].bitcast(U32).indirect(slots(g)))
+            turned = psum.tile([P, 4, P], F32, name=name + "t%d" % g, tag="turn%d" % g)
+            for t in range(4):
+                nc.tensor.transpose(turned[:, t, :], laid[:, t, :].bitcast(F32), ident[:])
+            cols = keep.tile([P, 4], F32, name=name + "c%d" % g)
+            nc.scalar.copy(cols[:], turned[:, :, ROW])
             return cols
 
-        kg = []
+        kg = [[keep.tile([P, 4, P], U32, name="kg%d%d" % (o, g), align_bytes=64) for g in range(G)] for o in range(O)]
 
-        def gather_keys(o, tags):
-            kg.append([keep.tile([P, 4, P], U32, name="kg%d%d" % (o, g), tag=tags[g], align_bytes=64) for g in range(G)])
-            for g in range(G):
-                nc.vector.tensor_copy(by_block(kg[o][g][:]), kw[o][:].bitcast(U32).indirect(slots(g)))
-
-        kbc = token_columns(kbw, "kb", "kbg")
+        kbc = [token_column(kbw, "kb", g, "kbg%d" % g) for g in range(G)]
         vw = [keep.tile([P, T], F32, name="vw0", tag="bias", align_bytes=64)]
-        nc.sync.dma_start(vw[0][:], vT[0:P, :])
-        gather_keys(0, ("kg00", "kg01"))
-        vsc = token_columns(vsw, "vs", "keys")
-        vw.append(keep.tile([P, T], F32, name="vw1", tag="scale", align_bytes=64))
-        nc.sync.dma_start(vw[1][:, 0:EARLY], vT[P:2 * P, 0:EARLY])
-        nc.sync.dma_start(vw[1][:, EARLY:T], vT[P:2 * P, EARLY:T])
-        gather_scales()
-        gather_keys(1, ("bytes", "kg11"))
+        load_window(vw[0], vT[0:P, :])
+        vsc = [token_column(vsw, "vs", 0, "vsg0")]
+        for g in range(G):
+            nc.vector.tensor_copy(by_block(kg[0][g][:]), kw[0][:].bitcast(U32).indirect(slots(g)))
+        vw.append(keep.tile([P, T], F32, name="vw1", tag="keys", align_bytes=64))
+        load_window(vw[1], vT[P:2 * P, :])
+        for g in range(G):
+            nc.vector.tensor_copy(by_block(kg[1][g][:]), window(kw[1], g).bitcast(U32).indirect(slots(g)))
+        vsc.append(token_column(vsw, "vs", 1, "logits"))
 
         rel = keep.tile([P, G, 4, NQ], F32, name="rel")
         prob = keep.tile([P, G, 4, NQ], F32, name="prob")
         for g in range(G):
-            score = psum.tile([P, 4, NQ], F32, name="score%d" % g)
-            for t in range(4):
-                for o in range(O):
+            score = [psum.tile([P, NQ], F32, name="score%d%d" % (g, t), tag="score%d" % t) for t in range(4)]
+            for o in range(O):
+                for t in range(4):
+                    first = g * PASS + t * P
                     nc.tensor.matmul_mx(
-                        out=score[:, t, :],
-                        lhsT=kg[o][g][:, t, :].bitcast(X4), lhsT_scale=ksp[4 * o:P, g, t, :],
-                        rhs=qw[:, o, :].bitcast(X4), rhs_scale=qs[4 * o:P, :],
+                        out=score[t][:],
+                        lhsT=kg[o][g][:, t, :].bitcast(X4), lhsT_scale=ksp[:, o, first:first + P],
+                        rhs=qw[:, o, :].bitcast(X4), rhs_scale=ksp[:, o, N:N + NQ],
                         start=(o == 0), stop=(o == O - 1))
             for t in range(4):
-                nc.scalar.activation(rel[:, g, t, :], score[:, t, :], ACT.Relu, bias=kbc[:, g, t:t + 1])
+                nc.scalar.activation(rel[:, g, t, :], score[t][:], ACT.Relu, bias=kbc[g][:, t:t + 1])
             nc.scalar.activation(prob[:, g], rel[:, g], ACT.Square)
 
-        vin = [[keep.tile([P, P, 4], BF16, name="vin%d%d" % (h, g), tag="vin%d%d" % (h, g), align_bytes=64) for g in range(G)] for h in range(H)]
+        vin = [[keep.tile([P, P, 4], BF16, name="vin%d%d" % (h, g), align_bytes=64) for g in range(G)] for h in range(H)]
         vq = [[keep.tile([P, P], U32, name="vq%d%d" % (h, g), align_bytes=64) for g in range(G)] for h in range(H)]
         vqs = [[keep.tile([P, P], U8, name="vqs%d%d" % (h, g), align_bytes=64) for g in range(G)] for h in range(H)]
 
         def gather_values(h, g):
-            window = vw[h][:, 0:EARLY] if (h, g) == (H - 1, 0) else vw[h][:]
             vb = keep.tile([P, 4, P], BF16, name="vb%d%d" % (h, g), align_bytes=64)
-            nc.vector.tensor_copy(by_block(vb[:]), window.indirect(slots(g)))
+            nc.vector.tensor_copy(by_block(vb[:]), window(vw[h], g).indirect(slots(g)))
             turned = psum.tile([P, 4, P], BF16, name="vt%d%d" % (h, g), tag="vt%d" % g)
             for t in range(4):
                 nc.tensor.transpose(turned[:, t, :], vb[:, t, :], identb[:])
@@ -159,47 +153,51 @@ def tile_attend_rel2_kb_gate_srtq128n1024t4096_kernel(tc, q_words, q_scales, k_w
         wq = [keep.tile([P, NQ], U32, name="wq%d" % g, align_bytes=64) for g in range(G)]
         wqs = [keep.tile([P, NQ], U8, name="wqs%d" % g, align_bytes=64) for g in range(G)]
 
-        def weigh(g):
-            nc.vector.tensor_tensor(wb[:, g], prob[:, g].rearrange("p t q -> p q t"), vsc[:, g, :].unsqueeze(1).to_broadcast([P, NQ, 4]), ALU.mult)
+        def weigh(g, wb):
+            nc.vector.tensor_tensor(wb[:].rearrange("p (c i) t -> p c t i", i=2),
+                                    prob[:, g].rearrange("p t (c i) -> p c t i", i=2),
+                                    vsc[g][:].unsqueeze(1).unsqueeze(3).to_broadcast([P, NQ // 2, 4, 2]), ALU.mult)
 
-        def quantize_weights(g):
-            nc.vector.quantize_mx(out=wq[g][:].bitcast(X4), scales=wqs[g][:], in_=wb[:, g].rearrange("p q t -> p (q t)"))
+        def quantize_weights(g, wb):
+            nc.vector.quantize_mx(out=wq[g][:].bitcast(X4), scales=wqs[g][:], in_=wb[:].rearrange("p q t -> p (q t)"))
 
+        wb0 = keep.tile([P, NQ, 4], BF16, name="wb0", align_bytes=64)
+        weigh(0, wb0)
         gather_values(0, 0)
+        quantize_weights(0, wb0)
         gather_values(0, 1)
-        wb = keep.tile([P, G, NQ, 4], BF16, name="wb", tag="bias", align_bytes=64)
-        weigh(0)
-        weigh(1)
-        quantize_weights(0)
+        late = keep.tile([P, NQ * 4 + 32], BF16, name="late", tag="bias", align_bytes=64)
+        wb1 = late[:, 0:NQ * 4].rearrange("p (q t) -> p q t", t=4)
+        inv = late[:, NQ * 4:NQ * 4 + 2].bitcast(F32)
+        weigh(1, wb1)
         quantize_values(0, 0)
-        quantize_weights(1)
-        quantize_values(0, 1)
 
-        back = psum.tile([P, P], F32, name="back", tag="vt1")
+        back = psum.tile([P, P], F32, name="back", tag="turn0")
         for i in range(4 * G):
             nc.tensor.matmul(back[:], prob[:, i // 4, i % 4, :], ident[:], start=(i == 0), stop=(i == 4 * G - 1), is_transpose=True)
         spare = keep.tile([P, P], F32, name="spare")
         total = keep.tile([P, 1], F32, name="total")
         nc.scalar.activation(spare[:], back[:], ACT.Copy, bias=1.0 / P, accum_out=total[:])
+        nc.vector.reciprocal(inv, total[:])
+        factor = keep.tile([P, DV], F32, name="factor")
+        nc.scalar.activation(factor[:], gate[:], ACT.Copy, scale=inv)
+        quantize_weights(1, wb1)
+        quantize_values(0, 1)
+
         gather_values(1, 0)
         gather_values(1, 1)
         quantize_values(1, 0)
-        quantize_values(1, 1)
 
-        inv = keep.tile([P, 1], F32, name="inv", tag="scale", align_bytes=64)
-        nc.vector.reciprocal(inv[:], total[:])
-        factor = keep.tile([P, DV], F32, name="factor")
-        nc.scalar.activation(factor[:], gate[:], ACT.Copy, scale=inv[:])
-
-        def finish(h):
-            y = psum.tile([P, P], F32, name="y%d" % h)
+        def finish(h, tag):
+            y = psum.tile([P, P], F32, name="y%d" % h, tag="score%d" % h)
             for g in range(G):
                 nc.tensor.matmul_mx(out=y[:], lhsT=wq[g][:].bitcast(X4), lhsT_scale=wqs[g][:],
                                     rhs=vq[h][g][:].bitcast(X4), rhs_scale=vqs[h][g][:],
                                     start=(g == 0), stop=(g == G - 1))
-            res = keep.tile([P, P], F32, name="res%d" % h)
+            res = keep.tile([P, P], F32, name="res%d" % h, tag=tag, align_bytes=64)
             nc.vector.tensor_tensor(res[:], y[:], factor[:, h * P:(h + 1) * P], ALU.mult)
             nc.sync.dma_start(out[0][:, h * P:(h + 1) * P], res[:])
 
-        finish(0)
-        finish(1)
+        finish(0, "keys")
+        quantize_values(1, 1)
+        finish(1, "res1")

@@ -25,6 +25,7 @@ H = DV // P
 ROW = P - 1
 EARLY = T - (N - PASS)
 RAW = 96
+ZEROED = 2048
 
 
 def tile_attend_rel2_kb_gate_srtq128n1024t4096_kernel(tc, q_words, q_scales, k_words, k_scales, vT, vs, kb, og, offs, out):
@@ -59,6 +60,7 @@ def tile_attend_rel2_kb_gate_srtq128n1024t4096_kernel(tc, q_words, q_scales, k_w
         kw = [keep.tile([P, T], I32, name="kw0", tag="keys", align_bytes=64)]
         qw = keep.tile([P, O, NQ], I32, name="qw", align_bytes=64)
         ksr = keep.tile([P, N + NQ], U8, name="ksr", align_bytes=64)
+        kbs = keep.tile([P, 32], F32, name="kbs")
         vss = keep.tile([P, 32], F32, name="vss")
         ksp = keep.tile([P, O, N + NQ], U8, name="ksp", align_bytes=64)
         ident = keep.tile([P, P], F32, name="ident")
@@ -67,22 +69,24 @@ def tile_attend_rel2_kb_gate_srtq128n1024t4096_kernel(tc, q_words, q_scales, k_w
         nc.sync.dma_start(ksw[RAW:P, :].bitcast(I32), k_scales.rearrange("o f t -> f o t").bitcast(I32))
         nc.sync.dma_start(kbw[ROW:P, :], kb[0:1, :])
         nc.sync.dma_start(ogt[:], og[0])
+        nc.sync.dma_start(kbs[:], kb[:, 0:32])
         nc.sync.dma_start(vss[:], vs[:, 0:32])
         nc.sync.dma_start(vsw[ROW:P, :], vs[0:1, :])
-        nc.sync.dma_start(ksr[RAW:P, N:N + NQ].bitcast(I32), q_scales[0].rearrange("o f q -> f o q").bitcast(I32))
         nc.sync.dma_start(kw[0][:], words(0))
+        nc.sync.dma_start(ksr[RAW:P, N:N + NQ].bitcast(I32), q_scales[0].rearrange("o f q -> f o q").bitcast(I32))
         nc.sync.dma_start(qw[:], q_words[0].rearrange("o g q r -> g o (q r)").bitcast(I32))
 
-        nc.gpsimd.memset(ksw[0:RAW, :].bitcast(I32), 0)
-        nc.gpsimd.memset(kbw[0:ROW, :], 0.0)
-        nc.vector.memset(ksp[:].rearrange("p o n -> p (o n)").bitcast(I32), 0)
         make_identity(nc, ident[:])
-        make_identity(nc, identb[:])
+        nc.vector.memset(ksw[0:RAW, :].bitcast(I32), 0)
+        nc.vector.memset(ksp[:].rearrange("p o n -> p (o n)").bitcast(I32), 0)
+        nc.vector.memset(kbw[0:ROW, 0:ZEROED], 0.0)
+        nc.vector.tensor_copy(identb[:], ident[:])
 
         gate = keep.tile([P, DV], F32, name="gate")
         nc.scalar.activation(gate[:], ogt[:], ACT.Sigmoid)
-        nc.scalar.activation(vsw[0:ROW, :].rearrange("p (a b) -> p a b", b=32),
-                             vss[0:ROW, :].unsqueeze(1).to_broadcast([ROW, T // 32, 32]), ACT.Copy)
+        for tile, source, first in ((kbw, kbs, ZEROED), (vsw, vss, 0)):
+            nc.scalar.activation(tile[0:ROW, first:T].rearrange("p (a b) -> p a b", b=32),
+                                 source[0:ROW, :].unsqueeze(1).to_broadcast([ROW, (T - first) // 32, 32]), ACT.Copy)
 
         ksg = keep.tile([P, N], U8, name="ksg", tag="logits", align_bytes=64)
         nc.vector.tensor_copy(ksg[:], ksw[:].indirect(offsets[:]))
@@ -109,9 +113,9 @@ def tile_attend_rel2_kb_gate_srtq128n1024t4096_kernel(tc, q_words, q_scales, k_w
         kbc = [token_column(kbw, "kb", g, "kbg%d" % g) for g in range(G)]
         vw = [keep.tile([P, T], F32, name="vw0", tag="bias", align_bytes=64)]
         load_window(vw[0], vT[0:P, :])
-        vsc = [token_column(vsw, "vs", 0, "vsg0")]
         for g in range(G):
             nc.vector.tensor_copy(by_block(kg[0][g][:]), kw[0][:].bitcast(U32).indirect(slots(g)))
+        vsc = [token_column(vsw, "vs", 0, "vsg0")]
         vw.append(keep.tile([P, T], F32, name="vw1", tag="keys", align_bytes=64))
         load_window(vw[1], vT[P:2 * P, :])
         for g in range(G):

@@ -32,6 +32,7 @@ def tile_attend_rel2_kb_gate_srtq128n1024t4096_kernel(tc, q_words, q_scales, k_w
     nc = tc.nc
     with ExitStack() as ctx:
         keep = ctx.enter_context(tc.tile_pool(name="keep", bufs=1))
+        reuse = ctx.enter_context(tc.tile_pool(name="reuse", bufs=1))
         psum = ctx.enter_context(tc.psum_pool(name="psum", bufs=1))
 
         offsets = keep.tile([P, N // 16], U16, name="offsets")
@@ -57,7 +58,8 @@ def tile_attend_rel2_kb_gate_srtq128n1024t4096_kernel(tc, q_words, q_scales, k_w
         vsw = keep.tile([P, T], F32, name="vsw", align_bytes=64)
         ksw = keep.tile([P, T], U8, name="ksw", align_bytes=64)
         ogt = keep.tile([P, DV], F32, name="ogt", align_bytes=64)
-        kw = [keep.tile([P, T], I32, name="kw0", tag="keys", align_bytes=64)]
+        kw = [reuse.tile([P, T], I32, name="kw0", offset=0, align_bytes=64),
+              keep.tile([P, T], I32, name="kw1", tag="keys1", align_bytes=64)]
         qw = keep.tile([P, O, NQ], I32, name="qw", align_bytes=64)
         ksr = keep.tile([P, N + NQ], U8, name="ksr", align_bytes=64)
         kbs = keep.tile([P, 32], F32, name="kbs")
@@ -75,12 +77,13 @@ def tile_attend_rel2_kb_gate_srtq128n1024t4096_kernel(tc, q_words, q_scales, k_w
         nc.sync.dma_start(kw[0][:], words(0))
         nc.sync.dma_start(ksr[RAW:P, N:N + NQ].bitcast(I32), q_scales[0].rearrange("o f q -> f o q").bitcast(I32))
         nc.sync.dma_start(qw[:], q_words[0].rearrange("o g q r -> g o (q r)").bitcast(I32))
+        load_window(kw[1], words(1))
 
+        nc.gpsimd.memset(ksp[:].rearrange("p o n -> p (o n)").bitcast(I32), 0)
         make_identity(nc, ident[:])
+        nc.gpsimd.tensor_copy(identb[:], ident[:])
         nc.vector.memset(ksw[0:RAW, :].bitcast(I32), 0)
-        nc.vector.memset(ksp[:].rearrange("p o n -> p (o n)").bitcast(I32), 0)
         nc.vector.memset(kbw[0:ROW, 0:ZEROED], 0.0)
-        nc.vector.tensor_copy(identb[:], ident[:])
 
         gate = keep.tile([P, DV], F32, name="gate")
         nc.scalar.activation(gate[:], ogt[:], ACT.Sigmoid)
@@ -88,19 +91,15 @@ def tile_attend_rel2_kb_gate_srtq128n1024t4096_kernel(tc, q_words, q_scales, k_w
             nc.scalar.activation(tile[0:ROW, first:T].rearrange("p (a b) -> p a b", b=32),
                                  source[0:ROW, :].unsqueeze(1).to_broadcast([ROW, (T - first) // 32, 32]), ACT.Copy)
 
-        ksg = keep.tile([P, N], U8, name="ksg", tag="logits", align_bytes=64)
+        ksg = keep.tile([P, N], U8, name="ksg")
         nc.vector.tensor_copy(ksg[:], ksw[:].indirect(offsets[:]))
         nc.vector.tensor_copy(
             ksr[RAW:P, 0:N].bitcast(I32).rearrange("p (g t b w) -> p g t b w", g=G, t=4, w=2),
             ksg[RAW:P, :].bitcast(I32).rearrange("p (g b t w) -> p g t b w", g=G, t=4, w=2))
         for q in range(4):
             nc.sync.dma_start(ksp[32 * q:32 * q + 4].bitcast(I32), ksr[RAW + 8 * q:RAW + 8 * q + 8, :].bitcast(I32))
-        kw.append(keep.tile([P, T], I32, name="kw1", tag="logits", align_bytes=64))
-        load_window(kw[1], words(1))
 
-        def token_column(source, name, g, tag):
-            laid = keep.tile([P, 4, P], U32, name=name + "g%d" % g, tag=tag, align_bytes=64)
-            nc.vector.tensor_copy(by_block(laid[:]), source[:].bitcast(U32).indirect(slots(g)))
+        def turn(laid, name, g):
             turned = psum.tile([P, 4, P], F32, name=name + "t%d" % g, tag="turn%d" % g)
             for t in range(4):
                 nc.tensor.transpose(turned[:, t, :], laid[:, t, :].bitcast(F32), ident[:])
@@ -108,26 +107,32 @@ def tile_attend_rel2_kb_gate_srtq128n1024t4096_kernel(tc, q_words, q_scales, k_w
             nc.scalar.copy(cols[:], turned[:, :, ROW])
             return cols
 
-        kg = [[keep.tile([P, 4, P], U32, name="kg%d%d" % (o, g), align_bytes=64) for g in range(G)] for o in range(O)]
+        def whole_list(ap):
+            return ap.rearrange("p g t (b r) -> p g b t r", r=8)
 
-        kbc = [token_column(kbw, "kb", g, "kbg%d" % g) for g in range(G)]
+        kg0 = keep.tile([P, G, 4, P], U32, name="kg0", align_bytes=64)
+        kg = [[kg0[:, g] for g in range(G)],
+              [keep.tile([P, 4, P], U32, name="kg1%d" % g, align_bytes=64)[:] for g in range(G)]]
+
+        kbg = keep.tile([P, G, 4, P], U32, name="kbg", align_bytes=64)
+        nc.vector.tensor_copy(whole_list(kbg[:]), kbw[:].bitcast(U32).indirect(offsets[:]))
+        kbc = [turn(kbg[:, g], "kb", g) for g in range(G)]
         vw = [keep.tile([P, T], F32, name="vw0", tag="bias", align_bytes=64)]
         load_window(vw[0], vT[0:P, :])
-        for g in range(G):
-            nc.vector.tensor_copy(by_block(kg[0][g][:]), kw[0][:].bitcast(U32).indirect(slots(g)))
-        vsc = [token_column(vsw, "vs", 0, "vsg0")]
-        vw.append(keep.tile([P, T], F32, name="vw1", tag="keys", align_bytes=64))
+        nc.vector.tensor_copy(whole_list(kg0[:]), kw[0][:].bitcast(U32).indirect(offsets[:]))
+        vw.append(reuse.tile([P, T], F32, name="vw1", offset=0, align_bytes=64))
         load_window(vw[1], vT[P:2 * P, :])
         for g in range(G):
-            nc.vector.tensor_copy(by_block(kg[1][g][:]), window(kw[1], g).bitcast(U32).indirect(slots(g)))
-        vsc.append(token_column(vsw, "vs", 1, "logits"))
+            nc.vector.tensor_copy(by_block(kg[1][g]), window(kw[1], g).bitcast(U32).indirect(slots(g)))
+        vsg = keep.tile([P, G, 4, P], U32, name="vsg", tag="keys1", align_bytes=64)
+        nc.vector.tensor_copy(whole_list(vsg[:]), vsw[:].bitcast(U32).indirect(offsets[:]))
 
         rel = keep.tile([P, G, 4, NQ], F32, name="rel")
         prob = keep.tile([P, G, 4, NQ], F32, name="prob")
         for g in range(G):
-            score = [psum.tile([P, NQ], F32, name="score%d%d" % (g, t), tag="score%d" % t) for t in range(4)]
-            for o in range(O):
-                for t in range(4):
+            score = [psum.tile([P, NQ], F32, name="score%d%d" % (g, t), tag="turn%d" % (t - 2) if g == 1 and t >= 2 else "score%d" % t) for t in range(4)]
+            for t in range(4):
+                for o in range(O):
                     first = g * PASS + t * P
                     nc.tensor.matmul_mx(
                         out=score[t][:],
@@ -137,10 +142,11 @@ def tile_attend_rel2_kb_gate_srtq128n1024t4096_kernel(tc, q_words, q_scales, k_w
             for t in range(4):
                 nc.scalar.activation(rel[:, g, t, :], score[t][:], ACT.Relu, bias=kbc[g][:, t:t + 1])
             nc.scalar.activation(prob[:, g], rel[:, g], ACT.Square)
+        vsc = [turn(vsg[:, g], "vs", g) for g in range(G)]
 
-        vin = [[keep.tile([P, P, 4], BF16, name="vin%d%d" % (h, g), align_bytes=64) for g in range(G)] for h in range(H)]
-        vq = [[keep.tile([P, P], U32, name="vq%d%d" % (h, g), align_bytes=64) for g in range(G)] for h in range(H)]
-        vqs = [[keep.tile([P, P], U8, name="vqs%d%d" % (h, g), align_bytes=64) for g in range(G)] for h in range(H)]
+        vin = [keep.tile([P, G, P, 4], BF16, name="vin%d" % h, align_bytes=64) for h in range(H)]
+        vq = [None, keep.tile([P, G, P], U32, name="vq1", align_bytes=64)]
+        vqs = [keep.tile([P, G, P], U8, name="vqs%d" % h, align_bytes=64) for h in range(H)]
 
         def gather_values(h, g):
             vb = keep.tile([P, 4, P], BF16, name="vb%d%d" % (h, g), align_bytes=64)
@@ -148,60 +154,56 @@ def tile_attend_rel2_kb_gate_srtq128n1024t4096_kernel(tc, q_words, q_scales, k_w
             turned = psum.tile([P, 4, P], BF16, name="vt%d%d" % (h, g), tag="vt%d" % g)
             for t in range(4):
                 nc.tensor.transpose(turned[:, t, :], vb[:, t, :], identb[:])
-            nc.scalar.copy(vin[h][g][:], turned[:].rearrange("p t e -> p e t"))
+            nc.scalar.copy(vin[h][:, g], turned[:].rearrange("p t e -> p e t"))
+
+        def quantize(codes, scales, values):
+            nc.vector.quantize_mx(out=codes.rearrange("p g c -> p (g c)").bitcast(X4), scales=scales.rearrange("p g c -> p (g c)"),
+                                  in_=values.rearrange("p g c t -> p (g c t)"))
 
         def quantize_values(h, g):
-            nc.vector.quantize_mx(out=vq[h][g][:].bitcast(X4), scales=vqs[h][g][:],
-                                  in_=vin[h][g][:].rearrange("p e t -> p (e t)"))
+            quantize(vq[h][:, g:g + 1], vqs[h][:, g:g + 1], vin[h][:, g:g + 1])
 
-        wq = [keep.tile([P, NQ], U32, name="wq%d" % g, align_bytes=64) for g in range(G)]
-        wqs = [keep.tile([P, NQ], U8, name="wqs%d" % g, align_bytes=64) for g in range(G)]
+        wq = keep.tile([P, G, NQ], U32, name="wq", align_bytes=64)
+        wqs = keep.tile([P, G, NQ], U8, name="wqs", align_bytes=64)
 
         def weigh(g, wb):
-            nc.vector.tensor_tensor(wb[:].rearrange("p (c i) t -> p c t i", i=2),
+            nc.vector.tensor_tensor(wb.rearrange("p (c i) t -> p c t i", i=2),
                                     prob[:, g].rearrange("p t (c i) -> p c t i", i=2),
                                     vsc[g][:].unsqueeze(1).unsqueeze(3).to_broadcast([P, NQ // 2, 4, 2]), ALU.mult)
 
-        def quantize_weights(g, wb):
-            nc.vector.quantize_mx(out=wq[g][:].bitcast(X4), scales=wqs[g][:], in_=wb[:].rearrange("p q t -> p (q t)"))
-
-        wb0 = keep.tile([P, NQ, 4], BF16, name="wb0", align_bytes=64)
-        weigh(0, wb0)
         gather_values(0, 0)
-        quantize_weights(0, wb0)
         gather_values(0, 1)
-        late = keep.tile([P, NQ * 4 + 32], BF16, name="late", tag="bias", align_bytes=64)
-        wb1 = late[:, 0:NQ * 4].rearrange("p (q t) -> p q t", t=4)
-        inv = late[:, NQ * 4:NQ * 4 + 2].bitcast(F32)
-        weigh(1, wb1)
-        quantize_values(0, 0)
+        wb = keep.tile([P, G, NQ, 4], BF16, name="wb", tag="bias", align_bytes=64)
+        for g in range(G):
+            weigh(g, wb[:, g])
+        quantize(wq[:], wqs[:], wb[:])
 
-        back = psum.tile([P, P], F32, name="back", tag="turn0")
+        back = psum.tile([P, P], F32, name="back", tag="score2")
         for i in range(4 * G):
             nc.tensor.matmul(back[:], prob[:, i // 4, i % 4, :], ident[:], start=(i == 0), stop=(i == 4 * G - 1), is_transpose=True)
         spare = keep.tile([P, P], F32, name="spare")
         total = keep.tile([P, 1], F32, name="total")
         nc.scalar.activation(spare[:], back[:], ACT.Copy, bias=1.0 / P, accum_out=total[:])
-        nc.vector.reciprocal(inv, total[:])
-        factor = keep.tile([P, DV], F32, name="factor")
-        nc.scalar.activation(factor[:], gate[:], ACT.Copy, scale=inv)
-        quantize_weights(1, wb1)
-        quantize_values(0, 1)
 
         gather_values(1, 0)
         gather_values(1, 1)
+        tail = reuse.tile([P, DV + 8], F32, name="tail", offset=0, align_bytes=64)
+        vq[0] = reuse.tile([P, G, P], U32, name="vq0", offset=2048, align_bytes=64)
+        inv = tail[:, DV:DV + 1]
+        nc.vector.reciprocal(inv, total[:])
+        quantize(vq[0][:], vqs[0][:], vin[0][:])
         quantize_values(1, 0)
 
-        def finish(h, tag):
+        def finish(h):
             y = psum.tile([P, P], F32, name="y%d" % h, tag="score%d" % h)
             for g in range(G):
-                nc.tensor.matmul_mx(out=y[:], lhsT=wq[g][:].bitcast(X4), lhsT_scale=wqs[g][:],
-                                    rhs=vq[h][g][:].bitcast(X4), rhs_scale=vqs[h][g][:],
+                nc.tensor.matmul_mx(out=y[:], lhsT=wq[:, g].bitcast(X4), lhsT_scale=wqs[:, g],
+                                    rhs=vq[h][:, g].bitcast(X4), rhs_scale=vqs[h][:, g],
                                     start=(g == 0), stop=(g == G - 1))
-            res = keep.tile([P, P], F32, name="res%d" % h, tag=tag, align_bytes=64)
-            nc.vector.tensor_tensor(res[:], y[:], factor[:, h * P:(h + 1) * P], ALU.mult)
-            nc.sync.dma_start(out[0][:, h * P:(h + 1) * P], res[:])
+            cols = slice(h * P, (h + 1) * P)
+            nc.vector.scalar_tensor_tensor(tail[:, cols], y[:], inv, gate[:, cols], ALU.mult, ALU.mult)
+            nc.sync.dma_start(out[0][:, cols], tail[:, cols])
 
-        finish(0, "keys")
+        finish(0)
         quantize_values(1, 1)
-        finish(1, "res1")
+        finish(1)

@@ -62,18 +62,17 @@ def tile_attend_rel2_kb_gate_srtq128n1024t4096_kernel(tc, q_words, q_scales, k_w
               keep.tile([P, T], I32, name="kw1", tag="keys1", align_bytes=64)]
         qw = keep.tile([P, O, NQ], I32, name="qw", align_bytes=64)
         ksr = keep.tile([P, N + NQ], U8, name="ksr", align_bytes=64)
-        kbs = keep.tile([P, 32], F32, name="kbs")
-        vss = keep.tile([P, 32], F32, name="vss")
+        kbs = keep.tile([P, (T - ZEROED) // P], F32, name="kbs")
+        vss = keep.tile([P, T // P], F32, name="vss")
         ksp = keep.tile([P, O, N + NQ], U8, name="ksp", align_bytes=64)
         ident = keep.tile([P, P], F32, name="ident")
         identb = keep.tile([P, P], BF16, name="identb")
 
         nc.sync.dma_start(ksw[RAW:P, :].bitcast(I32), k_scales.rearrange("o f t -> f o t").bitcast(I32))
-        nc.sync.dma_start(kbw[ROW:P, :], kb[0:1, :])
+        nc.sync.dma_start(kbw[ROW:P, 0:ZEROED], kb[0:1, 0:ZEROED])
         nc.sync.dma_start(ogt[:], og[0])
-        nc.sync.dma_start(kbs[:], kb[:, 0:32])
-        nc.sync.dma_start(vss[:], vs[:, 0:32])
-        nc.sync.dma_start(vsw[ROW:P, :], vs[0:1, :])
+        nc.sync.dma_start(kbs[:], kb[0, ZEROED:T].rearrange("(p c) -> p c", p=P))
+        nc.sync.dma_start(vss[:], vs[0].rearrange("(p c) -> p c", p=P))
         nc.sync.dma_start(kw[0][:], words(0))
         nc.sync.dma_start(ksr[RAW:P, N:N + NQ].bitcast(I32), q_scales[0].rearrange("o f q -> f o q").bitcast(I32))
         nc.sync.dma_start(qw[:], q_words[0].rearrange("o g q r -> g o (q r)").bitcast(I32))
@@ -87,9 +86,14 @@ def tile_attend_rel2_kb_gate_srtq128n1024t4096_kernel(tc, q_words, q_scales, k_w
 
         gate = keep.tile([P, DV], F32, name="gate")
         nc.scalar.activation(gate[:], ogt[:], ACT.Sigmoid)
-        for tile, source, first in ((kbw, kbs, ZEROED), (vsw, vss, 0)):
-            nc.scalar.activation(tile[0:ROW, first:T].rearrange("p (a b) -> p a b", b=32),
-                                 source[0:ROW, :].unsqueeze(1).to_broadcast([ROW, (T - first) // 32, 32]), ACT.Copy)
+        for name, tile, source, first in (("kb", kbw, kbs, ZEROED), ("vs", vsw, vss, 0)):
+            width = (T - first) // P
+            for k in range(width // 4):
+                spread = psum.tile([P, 4, P], F32, name=name + "s%d" % k, tag="score%d" % (k % 4))
+                for j in range(4):
+                    nc.tensor.transpose(spread[:, j, :], source[:, 4 * k + j:4 * k + j + 1].to_broadcast([P, P]), ident[:])
+                nc.scalar.activation(tile[:, first:T].rearrange("m (p c) -> m p c", c=width)[:, :, 4 * k:4 * k + 4],
+                                     spread[:].rearrange("m j p -> m p j"), ACT.Copy)
 
         ksg = keep.tile([P, N], U8, name="ksg")
         nc.vector.tensor_copy(ksg[:], ksw[:].indirect(offsets[:]))
@@ -120,17 +124,20 @@ def tile_attend_rel2_kb_gate_srtq128n1024t4096_kernel(tc, q_words, q_scales, k_w
         vw = [keep.tile([P, T], F32, name="vw0", tag="bias", align_bytes=64)]
         load_window(vw[0], vT[0:P, :])
         nc.vector.tensor_copy(whole_list(kg0[:]), kw[0][:].bitcast(U32).indirect(offsets[:]))
+        vsg0 = reuse.tile([P, 4, P], U32, name="vsg0", offset=0, align_bytes=64)
+        nc.vector.tensor_copy(by_block(vsg0[:]), vsw[:].bitcast(U32).indirect(slots(0)))
+        vsc = [turn(vsg0, "vs", 0)]
         vw.append(reuse.tile([P, T], F32, name="vw1", offset=0, align_bytes=64))
         load_window(vw[1], vT[P:2 * P, :])
         for g in range(G):
             nc.vector.tensor_copy(by_block(kg[1][g]), window(kw[1], g).bitcast(U32).indirect(slots(g)))
-        vsg = keep.tile([P, G, 4, P], U32, name="vsg", tag="keys1", align_bytes=64)
-        nc.vector.tensor_copy(whole_list(vsg[:]), vsw[:].bitcast(U32).indirect(offsets[:]))
+        vsg1 = keep.tile([P, 4, P], U32, name="vsg1", tag="keys1", align_bytes=64)
+        nc.vector.tensor_copy(by_block(vsg1[:]), vsw[:].bitcast(U32).indirect(slots(1)))
 
         rel = keep.tile([P, G, 4, NQ], F32, name="rel")
         prob = keep.tile([P, G, 4, NQ], F32, name="prob")
         for g in range(G):
-            score = [psum.tile([P, NQ], F32, name="score%d%d" % (g, t), tag="turn%d" % (t - 2) if g == 1 and t >= 2 else "score%d" % t) for t in range(4)]
+            score = [psum.tile([P, NQ], F32, name="score%d%d" % (g, t), tag="turn1" if (g, t) == (1, 3) else "score%d" % t) for t in range(4)]
             for t in range(4):
                 for o in range(O):
                     first = g * PASS + t * P
@@ -142,7 +149,7 @@ def tile_attend_rel2_kb_gate_srtq128n1024t4096_kernel(tc, q_words, q_scales, k_w
             for t in range(4):
                 nc.scalar.activation(rel[:, g, t, :], score[t][:], ACT.Relu, bias=kbc[g][:, t:t + 1])
             nc.scalar.activation(prob[:, g], rel[:, g], ACT.Square)
-        vsc = [turn(vsg[:, g], "vs", g) for g in range(G)]
+        vsc.append(turn(vsg1, "vs", 1))
 
         vin = [keep.tile([P, G, P, 4], BF16, name="vin%d" % h, align_bytes=64) for h in range(H)]
         vq = [None, keep.tile([P, G, P], U32, name="vq1", align_bytes=64)]

@@ -42,7 +42,7 @@ def tile_attend_rel2_kb_gate_srtq128n1024t4096_kernel(tc, q_words, q_scales, k_w
             return offsets[:, g * (PASS // 16):(g + 1) * (PASS // 16)]
 
         def by_block(ap):
-            return ap.rearrange("p t (b r) -> p b t r", r=8)
+            return ap.rearrange("p t (a r) -> p a t r", r=4)
 
         def words(o):
             return k_words[o].rearrange("g t r -> g (t r)").bitcast(I32)
@@ -62,17 +62,17 @@ def tile_attend_rel2_kb_gate_srtq128n1024t4096_kernel(tc, q_words, q_scales, k_w
               keep.tile([P, T], I32, name="kw1", tag="keys1", align_bytes=64)]
         qw = keep.tile([P, O, NQ], I32, name="qw", align_bytes=64)
         ksr = keep.tile([P, N + NQ], U8, name="ksr", align_bytes=64)
-        kbs = keep.tile([P, (T - ZEROED) // P], F32, name="kbs")
-        vss = keep.tile([P, T // P], F32, name="vss")
+        kbs = keep.tile([P, 32], F32, name="kbs")
+        vss = keep.tile([P, 32], F32, name="vss")
         ksp = keep.tile([P, O, N + NQ], U8, name="ksp", align_bytes=64)
         ident = keep.tile([P, P], F32, name="ident")
-        identb = keep.tile([P, P], BF16, name="identb")
 
         nc.sync.dma_start(ksw[RAW:P, :].bitcast(I32), k_scales.rearrange("o f t -> f o t").bitcast(I32))
-        nc.sync.dma_start(kbw[ROW:P, 0:ZEROED], kb[0:1, 0:ZEROED])
+        nc.sync.dma_start(kbw[ROW:P, :], kb[0:1, :])
         nc.sync.dma_start(ogt[:], og[0])
-        nc.sync.dma_start(kbs[:], kb[0, ZEROED:T].rearrange("(p c) -> p c", p=P))
-        nc.sync.dma_start(vss[:], vs[0].rearrange("(p c) -> p c", p=P))
+        nc.sync.dma_start(kbs[:], kb[:, 0:32])
+        nc.sync.dma_start(vss[:], vs[:, 0:32])
+        nc.sync.dma_start(vsw[ROW:P, :], vs[0:1, :])
         nc.sync.dma_start(kw[0][:], words(0))
         nc.sync.dma_start(ksr[RAW:P, N:N + NQ].bitcast(I32), q_scales[0].rearrange("o f q -> f o q").bitcast(I32))
         nc.sync.dma_start(qw[:], q_words[0].rearrange("o g q r -> g o (q r)").bitcast(I32))
@@ -80,26 +80,20 @@ def tile_attend_rel2_kb_gate_srtq128n1024t4096_kernel(tc, q_words, q_scales, k_w
 
         nc.gpsimd.memset(ksp[:].rearrange("p o n -> p (o n)").bitcast(I32), 0)
         make_identity(nc, ident[:])
-        nc.gpsimd.tensor_copy(identb[:], ident[:])
         nc.vector.memset(ksw[0:RAW, :].bitcast(I32), 0)
         nc.vector.memset(kbw[0:ROW, 0:ZEROED], 0.0)
 
         gate = keep.tile([P, DV], F32, name="gate")
         nc.scalar.activation(gate[:], ogt[:], ACT.Sigmoid)
-        for name, tile, source, first in (("kb", kbw, kbs, ZEROED), ("vs", vsw, vss, 0)):
-            width = (T - first) // P
-            for k in range(width // 4):
-                spread = psum.tile([P, 4, P], F32, name=name + "s%d" % k, tag="score%d" % (k % 4))
-                for j in range(4):
-                    nc.tensor.transpose(spread[:, j, :], source[:, 4 * k + j:4 * k + j + 1].to_broadcast([P, P]), ident[:])
-                nc.scalar.activation(tile[:, first:T].rearrange("m (p c) -> m p c", c=width)[:, :, 4 * k:4 * k + 4],
-                                     spread[:].rearrange("m j p -> m p j"), ACT.Copy)
+        for tile, source, first in ((kbw, kbs, ZEROED), (vsw, vss, 0)):
+            nc.scalar.activation(tile[0:ROW, first:T].rearrange("p (a b) -> p a b", b=32),
+                                 source[0:ROW, :].unsqueeze(1).to_broadcast([ROW, (T - first) // 32, 32]), ACT.Copy)
 
         ksg = keep.tile([P, N], U8, name="ksg")
         nc.vector.tensor_copy(ksg[:], ksw[:].indirect(offsets[:]))
         nc.vector.tensor_copy(
-            ksr[RAW:P, 0:N].bitcast(I32).rearrange("p (g t b w) -> p g t b w", g=G, t=4, w=2),
-            ksg[RAW:P, :].bitcast(I32).rearrange("p (g b t w) -> p g t b w", g=G, t=4, w=2))
+            ksr[RAW:P, 0:N].bitcast(I32).rearrange("p (g t a) -> p g t a", g=G, t=4),
+            ksg[RAW:P, :].bitcast(I32).rearrange("p (g a t) -> p g t a", g=G, t=4))
         for q in range(4):
             nc.sync.dma_start(ksp[32 * q:32 * q + 4].bitcast(I32), ksr[RAW + 8 * q:RAW + 8 * q + 8, :].bitcast(I32))
 
@@ -112,7 +106,7 @@ def tile_attend_rel2_kb_gate_srtq128n1024t4096_kernel(tc, q_words, q_scales, k_w
             return cols
 
         def whole_list(ap):
-            return ap.rearrange("p g t (b r) -> p g b t r", r=8)
+            return ap.rearrange("p g t (a r) -> p g a t r", r=4)
 
         kg0 = keep.tile([P, G, 4, P], U32, name="kg0", align_bytes=64)
         kg = [[kg0[:, g] for g in range(G)],
@@ -151,17 +145,17 @@ def tile_attend_rel2_kb_gate_srtq128n1024t4096_kernel(tc, q_words, q_scales, k_w
             nc.scalar.activation(prob[:, g], rel[:, g], ACT.Square)
         vsc.append(turn(vsg1, "vs", 1))
 
-        vin = [keep.tile([P, G, P, 4], BF16, name="vin%d" % h, align_bytes=64) for h in range(H)]
+        vin = [keep.tile([P, G, P, 4], BF16, name="vin%d" % h, tag="vin%d" % h, align_bytes=64) for h in range(H)]
         vq = [None, keep.tile([P, G, P], U32, name="vq1", align_bytes=64)]
         vqs = [keep.tile([P, G, P], U8, name="vqs%d" % h, align_bytes=64) for h in range(H)]
 
         def gather_values(h, g):
-            vb = keep.tile([P, 4, P], BF16, name="vb%d%d" % (h, g), align_bytes=64)
-            nc.vector.tensor_copy(by_block(vb[:]), window(vw[h], g).indirect(slots(g)))
-            turned = psum.tile([P, 4, P], BF16, name="vt%d%d" % (h, g), tag="vt%d" % g)
-            for t in range(4):
-                nc.tensor.transpose(turned[:, t, :], vb[:, t, :], identb[:])
-            nc.scalar.copy(vin[h][:, g], turned[:].rearrange("p t e -> p e t"))
+            vb = keep.tile([P, 2, P, 2], BF16, name="vb%d%d" % (h, g), align_bytes=64)
+            nc.vector.tensor_copy(vb[:].rearrange("p u (a r) s -> p a u s r", r=4), window(vw[h], g).indirect(slots(g)))
+            turned = psum.tile([P, 2, P], F32, name="vt%d%d" % (h, g), tag="vt%d" % g)
+            for u in range(2):
+                nc.tensor.transpose(turned[:, u, :], vb[:, u].rearrange("p c s -> p (c s)").bitcast(F32), ident[:])
+            nc.scalar.copy(vin[h][:, g].bitcast(F32), turned[:].rearrange("p u e -> p e u"))
 
         def quantize(codes, scales, values):
             nc.vector.quantize_mx(out=codes.rearrange("p g c -> p (g c)").bitcast(X4), scales=scales.rearrange("p g c -> p (g c)"),
@@ -194,12 +188,13 @@ def tile_attend_rel2_kb_gate_srtq128n1024t4096_kernel(tc, q_words, q_scales, k_w
 
         gather_values(1, 0)
         gather_values(1, 1)
-        tail = reuse.tile([P, DV + 8], F32, name="tail", offset=0, align_bytes=64)
+        inv = reuse.tile([P, 1], F32, name="inv", offset=0, align_bytes=64)
         vq[0] = reuse.tile([P, G, P], U32, name="vq0", offset=2048, align_bytes=64)
-        inv = tail[:, DV:DV + 1]
-        nc.vector.reciprocal(inv, total[:])
+        nc.vector.reciprocal(inv[:], total[:])
         quantize(vq[0][:], vqs[0][:], vin[0][:])
         quantize_values(1, 0)
+        quantize_values(1, 1)
+        res = keep.tile([P, DV], F32, name="res", tag="vin1", align_bytes=64)
 
         def finish(h):
             y = psum.tile([P, P], F32, name="y%d" % h, tag="score%d" % h)
@@ -208,9 +203,8 @@ def tile_attend_rel2_kb_gate_srtq128n1024t4096_kernel(tc, q_words, q_scales, k_w
                                     rhs=vq[h][:, g].bitcast(X4), rhs_scale=vqs[h][:, g],
                                     start=(g == 0), stop=(g == G - 1))
             cols = slice(h * P, (h + 1) * P)
-            nc.vector.scalar_tensor_tensor(tail[:, cols], y[:], inv, gate[:, cols], ALU.mult, ALU.mult)
-            nc.sync.dma_start(out[0][:, cols], tail[:, cols])
+            nc.vector.scalar_tensor_tensor(res[:, cols], y[:], inv[:], gate[:, cols], ALU.mult, ALU.mult)
+            nc.sync.dma_start(out[0][:, cols], res[:, cols])
 
         finish(0)
-        quantize_values(1, 1)
         finish(1)

@@ -24,8 +24,9 @@ O = D // PASS
 H = DV // P
 ROW = P - 1
 EARLY = T - (N - PASS)
-RAW = 96
-ZEROED = 2048
+RAW = 32
+RAW_END = RAW + 32
+ZEROED = 1536
 
 
 def tile_attend_rel2_kb_gate_srtq128n1024t4096_kernel(tc, q_words, q_scales, k_words, k_scales, vT, vs, kb, og, offs, out):
@@ -67,20 +68,21 @@ def tile_attend_rel2_kb_gate_srtq128n1024t4096_kernel(tc, q_words, q_scales, k_w
         ksp = keep.tile([P, O, N + NQ], U8, name="ksp", align_bytes=64)
         ident = keep.tile([P, P], F32, name="ident")
 
-        nc.sync.dma_start(ksw[RAW:P, :].bitcast(I32), k_scales.rearrange("o f t -> f o t").bitcast(I32))
+        nc.sync.dma_start(ksw[RAW:RAW_END, :].bitcast(I32), k_scales.rearrange("o f t -> f o t").bitcast(I32))
         nc.sync.dma_start(kbw[ROW:P, :], kb[0:1, :])
         nc.sync.dma_start(ogt[:], og[0])
         nc.sync.dma_start(kbs[:], kb[:, 0:32])
         nc.sync.dma_start(vss[:], vs[:, 0:32])
         nc.sync.dma_start(vsw[ROW:P, :], vs[0:1, :])
         nc.sync.dma_start(kw[0][:], words(0))
-        nc.sync.dma_start(ksr[RAW:P, N:N + NQ].bitcast(I32), q_scales[0].rearrange("o f q -> f o q").bitcast(I32))
+        nc.sync.dma_start(ksr[RAW:RAW_END, N:N + NQ].bitcast(I32), q_scales[0].rearrange("o f q -> f o q").bitcast(I32))
         nc.sync.dma_start(qw[:], q_words[0].rearrange("o g q r -> g o (q r)").bitcast(I32))
         load_window(kw[1], words(1))
 
         nc.gpsimd.memset(ksp[:].rearrange("p o n -> p (o n)").bitcast(I32), 0)
         make_identity(nc, ident[:])
         nc.vector.memset(ksw[0:RAW, :].bitcast(I32), 0)
+        nc.vector.memset(ksw[RAW_END:P, :].bitcast(I32), 0)
         nc.vector.memset(kbw[0:ROW, 0:ZEROED], 0.0)
 
         gate = keep.tile([P, DV], F32, name="gate")
@@ -92,8 +94,8 @@ def tile_attend_rel2_kb_gate_srtq128n1024t4096_kernel(tc, q_words, q_scales, k_w
         ksg = keep.tile([P, N], U8, name="ksg")
         nc.vector.tensor_copy(ksg[:], ksw[:].indirect(offsets[:]))
         nc.vector.tensor_copy(
-            ksr[RAW:P, 0:N].bitcast(I32).rearrange("p (g t a) -> p g t a", g=G, t=4),
-            ksg[RAW:P, :].bitcast(I32).rearrange("p (g a t) -> p g t a", g=G, t=4))
+            ksr[RAW:RAW_END, 0:N].bitcast(I32).rearrange("p (g t a) -> p g t a", g=G, t=4),
+            ksg[RAW:RAW_END, :].bitcast(I32).rearrange("p (g a t) -> p g t a", g=G, t=4))
         for q in range(4):
             nc.sync.dma_start(ksp[32 * q:32 * q + 4].bitcast(I32), ksr[RAW + 8 * q:RAW + 8 * q + 8, :].bitcast(I32))
 

@@ -26,7 +26,7 @@ ROW = P - 1
 EARLY = T - (N - PASS)
 RAW = 32
 RAW_END = RAW + 32
-ZEROED = 1536
+ZEROED = 1920
 
 
 def tile_attend_rel2_kb_gate_srtq128n1024t4096_kernel(tc, q_words, q_scales, k_words, k_scales, vT, vs, kb, og, offs, out):
@@ -68,12 +68,12 @@ def tile_attend_rel2_kb_gate_srtq128n1024t4096_kernel(tc, q_words, q_scales, k_w
         ksp = keep.tile([P, O, N + NQ], U8, name="ksp", align_bytes=64)
         ident = keep.tile([P, P], F32, name="ident")
 
-        nc.sync.dma_start(ksw[RAW:RAW_END, :].bitcast(I32), k_scales.rearrange("o f t -> f o t").bitcast(I32))
         nc.sync.dma_start(kbw[ROW:P, :], kb[0:1, :])
+        nc.sync.dma_start(ksw[RAW:RAW_END, :].bitcast(I32), k_scales.rearrange("o f t -> f o t").bitcast(I32))
+        nc.sync.dma_start(vsw[ROW:P, :], vs[0:1, :])
         nc.sync.dma_start(ogt[:], og[0])
         nc.sync.dma_start(kbs[:], kb[:, 0:32])
         nc.sync.dma_start(vss[:], vs[:, 0:32])
-        nc.sync.dma_start(vsw[ROW:P, :], vs[0:1, :])
         nc.sync.dma_start(kw[0][:], words(0))
         nc.sync.dma_start(ksr[RAW:RAW_END, N:N + NQ].bitcast(I32), q_scales[0].rearrange("o f q -> f o q").bitcast(I32))
         nc.sync.dma_start(qw[:], q_words[0].rearrange("o g q r -> g o (q r)").bitcast(I32))

@@ -1,7 +1,6 @@
 from contextlib import ExitStack
 
 import concourse.mybir as mybir
-from concourse.masks import make_identity
 
 N, T, D, DV, NQ = 1024, 4096, 1024, 256, 128
 FLOPS = 2 * NQ * N * D + 2 * NQ * N * DV
@@ -26,7 +25,7 @@ ROW = P - 1
 EARLY = T - (N - PASS)
 RAW = 32
 RAW_END = RAW + 32
-ZEROED = 1920
+ZEROED = 1408
 
 
 def tile_attend_rel2_kb_gate_srtq128n1024t4096_kernel(tc, q_words, q_scales, k_words, k_scales, vT, vs, kb, og, offs, out):
@@ -58,7 +57,6 @@ def tile_attend_rel2_kb_gate_srtq128n1024t4096_kernel(tc, q_words, q_scales, k_w
         kbw = keep.tile([P, T], F32, name="kbw", tag="bias", align_bytes=64)
         vsw = keep.tile([P, T], F32, name="vsw", align_bytes=64)
         ksw = keep.tile([P, T], U8, name="ksw", align_bytes=64)
-        ogt = keep.tile([P, DV], F32, name="ogt", align_bytes=64)
         kw = [reuse.tile([P, T], I32, name="kw0", offset=0, align_bytes=64),
               keep.tile([P, T], I32, name="kw1", tag="keys1", align_bytes=64)]
         qw = keep.tile([P, O, NQ], I32, name="qw", align_bytes=64)
@@ -68,25 +66,24 @@ def tile_attend_rel2_kb_gate_srtq128n1024t4096_kernel(tc, q_words, q_scales, k_w
         ksp = keep.tile([P, O, N + NQ], U8, name="ksp", align_bytes=64)
         ident = keep.tile([P, P], F32, name="ident")
 
-        nc.sync.dma_start(kbw[ROW:P, :], kb[0:1, :])
         nc.sync.dma_start(ksw[RAW:RAW_END, :].bitcast(I32), k_scales.rearrange("o f t -> f o t").bitcast(I32))
-        nc.sync.dma_start(vsw[ROW:P, :], vs[0:1, :])
-        nc.sync.dma_start(ogt[:], og[0])
         nc.sync.dma_start(kbs[:], kb[:, 0:32])
+        nc.sync.dma_start(kbw[ROW:P, :], kb[0:1, :])
         nc.sync.dma_start(vss[:], vs[:, 0:32])
         nc.sync.dma_start(kw[0][:], words(0))
+        nc.sync.dma_start(vsw[ROW:P, :], vs[0:1, :])
         nc.sync.dma_start(ksr[RAW:RAW_END, N:N + NQ].bitcast(I32), q_scales[0].rearrange("o f q -> f o q").bitcast(I32))
-        nc.sync.dma_start(qw[:], q_words[0].rearrange("o g q r -> g o (q r)").bitcast(I32))
         load_window(kw[1], words(1))
+        nc.sync.dma_start(qw[:], q_words[0].rearrange("o g q r -> g o (q r)").bitcast(I32))
 
-        nc.gpsimd.memset(ksp[:].rearrange("p o n -> p (o n)").bitcast(I32), 0)
-        make_identity(nc, ident[:])
+        ramp = keep.tile([P, P], F32, name="ramp")
+        nc.gpsimd.iota(ramp[:], [[1, P]], base=0, channel_multiplier=-1, allow_small_or_imprecise_dtypes=True)
         nc.vector.memset(ksw[0:RAW, :].bitcast(I32), 0)
         nc.vector.memset(ksw[RAW_END:P, :].bitcast(I32), 0)
+        nc.vector.memset(ksp[:].rearrange("p o n -> p (o n)").bitcast(I32), 0)
+        nc.vector.tensor_scalar(ident[:], ramp[:], 0.0, None, ALU.is_equal)
         nc.vector.memset(kbw[0:ROW, 0:ZEROED], 0.0)
 
-        gate = keep.tile([P, DV], F32, name="gate")
-        nc.scalar.activation(gate[:], ogt[:], ACT.Sigmoid)
         for tile, source, first in ((kbw, kbs, ZEROED), (vsw, vss, 0)):
             nc.scalar.activation(tile[0:ROW, first:T].rearrange("p (a b) -> p a b", b=32),
                                  source[0:ROW, :].unsqueeze(1).to_broadcast([ROW, (T - first) // 32, 32]), ACT.Copy)
@@ -120,11 +117,14 @@ def tile_attend_rel2_kb_gate_srtq128n1024t4096_kernel(tc, q_words, q_scales, k_w
         vw = [keep.tile([P, T], F32, name="vw0", tag="bias", align_bytes=64)]
         load_window(vw[0], vT[0:P, :])
         nc.vector.tensor_copy(whole_list(kg0[:]), kw[0][:].bitcast(U32).indirect(offsets[:]))
-        vsg0 = reuse.tile([P, 4, P], U32, name="vsg0", offset=0, align_bytes=64)
+        vsg0 = reuse.tile([P, 4, P], U32, name="vsg0", offset=4 * T - 4 * DV, align_bytes=64)
         nc.vector.tensor_copy(by_block(vsg0[:]), vsw[:].bitcast(U32).indirect(slots(0)))
         vsc = [turn(vsg0, "vs", 0)]
         vw.append(reuse.tile([P, T], F32, name="vw1", offset=0, align_bytes=64))
-        load_window(vw[1], vT[P:2 * P, :])
+        ogt = reuse.tile([P, DV], F32, name="ogt", offset=4 * T, align_bytes=64)
+        nc.sync.dma_start(vw[1][:, 0:EARLY], vT[P:2 * P, 0:EARLY])
+        nc.sync.dma_start(ogt[:], og[0])
+        nc.sync.dma_start(vw[1][:, EARLY:T], vT[P:2 * P, EARLY:T])
         for g in range(G):
             nc.vector.tensor_copy(by_block(kg[1][g]), window(kw[1], g).bitcast(U32).indirect(slots(g)))
         vsg1 = keep.tile([P, 4, P], U32, name="vsg1", tag="keys1", align_bytes=64)
@@ -188,6 +188,10 @@ def tile_attend_rel2_kb_gate_srtq128n1024t4096_kernel(tc, q_words, q_scales, k_w
         total = keep.tile([P, 1], F32, name="total")
         nc.scalar.activation(spare[:], back[:], ACT.Copy, bias=1.0 / P, accum_out=total[:])
 
+        half = keep.tile([P, DV], F32, name="half")
+        gate = keep.tile([P, DV], F32, name="gate")
+        nc.scalar.activation(half[:], ogt[:], ACT.Tanh, scale=0.5)
+        nc.scalar.activation(gate[:], half[:], ACT.Copy, scale=0.5, bias=0.5)
         gather_values(1, 0)
         gather_values(1, 1)
         inv = reuse.tile([P, 1], F32, name="inv", offset=0, align_bytes=64)

@@ -21,11 +21,15 @@ PASS = 512
 G = N // PASS
 O = D // PASS
 H = DV // P
-ROW = P - 1
+KB_ROW = P - 1
+VS_ROW = P - 1
 EARLY = T - (N - PASS)
+SHARE = 352
 RAW = 32
 RAW_END = RAW + 32
 ZEROED = 1408
+AHEAD = 3
+WINDOW = 4 * T
 
 
 def tile_attend_rel2_kb_gate_srtq128n1024t4096_kernel(tc, q_words, q_scales, k_words, k_scales, vT, vs, kb, og, offs, out):
@@ -35,175 +39,197 @@ def tile_attend_rel2_kb_gate_srtq128n1024t4096_kernel(tc, q_words, q_scales, k_w
         reuse = ctx.enter_context(tc.tile_pool(name="reuse", bufs=1))
         psum = ctx.enter_context(tc.psum_pool(name="psum", bufs=1))
 
-        offsets = keep.tile([P, N // 16], U16, name="offsets")
-        nc.sync.dma_start(offsets[:], offs)
-
-        def slots(g):
-            return offsets[:, g * (PASS // 16):(g + 1) * (PASS // 16)]
-
-        def by_block(ap):
-            return ap.rearrange("p t (a r) -> p a t r", r=4)
-
         def words(o):
             return k_words[o].rearrange("g t r -> g (t r)").bitcast(I32)
 
-        def load_window(tile, source):
-            nc.sync.dma_start(tile[:, 0:EARLY], source[:, 0:EARLY])
-            nc.sync.dma_start(tile[:, EARLY:T], source[:, EARLY:T])
-
-        def window(tile, g):
-            return tile[:, 0:EARLY] if g == 0 else tile[:]
-
-        kbw = keep.tile([P, T], F32, name="kbw", tag="bias", align_bytes=64)
-        vsw = keep.tile([P, T], F32, name="vsw", align_bytes=64)
-        ksw = keep.tile([P, T], U8, name="ksw", align_bytes=64)
-        kw = [reuse.tile([P, T], I32, name="kw0", offset=0, align_bytes=64),
-              keep.tile([P, T], I32, name="kw1", tag="keys1", align_bytes=64)]
+        offsets = keep.tile([P, N // 16], U16, name="offsets")
+        kbw = reuse.tile([P, T], F32, name="kbw", offset=5 * WINDOW, align_bytes=64)
+        kw0 = reuse.tile([P, T], I32, name="kw0", offset=0, align_bytes=64)
+        ramp = keep.tile([P, P], F32, name="ramp")
+        kbs = keep.tile([P, 32], F32, name="kbs")
+        ksw = reuse.tile([P, T], U8, name="ksw", offset=3 * WINDOW, align_bytes=64)
         qw = keep.tile([P, O, NQ], I32, name="qw", align_bytes=64)
         ksr = keep.tile([P, N + NQ], U8, name="ksr", align_bytes=64)
-        kbs = keep.tile([P, 32], F32, name="kbs")
-        vss = keep.tile([P, 32], F32, name="vss")
-        ksp = keep.tile([P, O, N + NQ], U8, name="ksp", align_bytes=64)
+        ksp = keep.tile([P, N + NQ], U8, name="ksp", align_bytes=64)
         ident = keep.tile([P, P], F32, name="ident")
 
-        nc.sync.dma_start(ksw[RAW:RAW_END, :].bitcast(I32), k_scales.rearrange("o f t -> f o t").bitcast(I32))
-        nc.sync.dma_start(kbs[:], kb[:, 0:32])
-        nc.sync.dma_start(kbw[ROW:P, :], kb[0:1, :])
-        nc.sync.dma_start(vss[:], vs[:, 0:32])
-        nc.sync.dma_start(kw[0][:], words(0))
-        nc.sync.dma_start(vsw[ROW:P, :], vs[0:1, :])
-        nc.sync.dma_start(ksr[RAW:RAW_END, N:N + NQ].bitcast(I32), q_scales[0].rearrange("o f q -> f o q").bitcast(I32))
-        load_window(kw[1], words(1))
-        nc.sync.dma_start(qw[:], q_words[0].rearrange("o g q r -> g o (q r)").bitcast(I32))
+        def slots(first, count):
+            return offsets[:, first // 16:(first + count) // 16]
 
-        ramp = keep.tile([P, P], F32, name="ramp")
+        def slot_order(ap, g):
+            if g == 0:
+                return ap.rearrange("p t (a r) -> p a t r", r=4)
+            return ap.rearrange("p t c -> p c t")
+
         nc.gpsimd.iota(ramp[:], [[1, P]], base=0, channel_multiplier=-1, allow_small_or_imprecise_dtypes=True)
         nc.vector.memset(ksw[0:RAW, :].bitcast(I32), 0)
         nc.vector.memset(ksw[RAW_END:P, :].bitcast(I32), 0)
-        nc.vector.memset(ksp[:].rearrange("p o n -> p (o n)").bitcast(I32), 0)
         nc.vector.tensor_scalar(ident[:], ramp[:], 0.0, None, ALU.is_equal)
-        nc.vector.memset(kbw[0:ROW, 0:ZEROED], 0.0)
+        nc.vector.memset(ksp[:].bitcast(I32), 0)
+        nc.vector.memset(kbw[0:KB_ROW, 0:ZEROED], 0.0)
 
-        for tile, source, first in ((kbw, kbs, ZEROED), (vsw, vss, 0)):
-            nc.scalar.activation(tile[0:ROW, first:T].rearrange("p (a b) -> p a b", b=32),
-                                 source[0:ROW, :].unsqueeze(1).to_broadcast([ROW, (T - first) // 32, 32]), ACT.Copy)
+        nc.sync.dma_start(ksw[RAW:RAW_END, :].bitcast(I32), k_scales.rearrange("o f t -> (o f) t").bitcast(I32))
+        nc.sync.dma_start(offsets[:], offs)
+        nc.sync.dma_start(kbs[:], kb[:, 0:32])
+        nc.sync.dma_start(kbw[KB_ROW:P, :], kb[0:1, :])
+        nc.sync.dma_start(ksr[RAW:RAW_END, N:N + NQ].bitcast(I32), q_scales[0].rearrange("o f q -> (o f) q").bitcast(I32))
+        nc.sync.dma_start(qw[:], q_words[0].rearrange("o g q r -> g o (q r)").bitcast(I32))
+        nc.sync.dma_start(kw0[:], words(0))
 
-        ksg = keep.tile([P, N], U8, name="ksg")
-        nc.vector.tensor_copy(ksg[:], ksw[:].indirect(offsets[:]))
-        nc.vector.tensor_copy(
-            ksr[RAW:RAW_END, 0:N].bitcast(I32).rearrange("p (g t a) -> p g t a", g=G, t=4),
-            ksg[RAW:RAW_END, :].bitcast(I32).rearrange("p (g a t) -> p g t a", g=G, t=4))
-        for q in range(4):
-            nc.sync.dma_start(ksp[32 * q:32 * q + 4].bitcast(I32), ksr[RAW + 8 * q:RAW + 8 * q + 8, :].bitcast(I32))
+        nc.scalar.activation(kbw[0:KB_ROW, ZEROED:T].rearrange("p (a b) -> p a b", b=32),
+                             kbs[0:KB_ROW, :].unsqueeze(1).to_broadcast([KB_ROW, (T - ZEROED) // 32, 32]), ACT.Copy)
 
-        def turn(laid, name, g):
-            turned = psum.tile([P, 4, P], F32, name=name + "t%d" % g, tag="turn%d" % g)
+        ksg = reuse.tile([P, N], U8, name="ksg", offset=2 * WINDOW - PASS, align_bytes=64)
+        for g in (1, 0):
+            nc.vector.tensor_copy(ksg[:, g * PASS:(g + 1) * PASS], ksw[:].indirect(slots(g * PASS, PASS)))
+        nc.vector.tensor_copy(ksr[:, PASS:N].rearrange("p (t c) -> p t c", t=4),
+                              ksg[:, PASS:N].rearrange("p (c t) -> p t c", t=4))
+        nc.vector.tensor_copy(ksr[RAW:RAW_END, 0:PASS].bitcast(I32).rearrange("p (t a) -> p t a", t=4),
+                              ksg[RAW:RAW_END, 0:PASS].bitcast(I32).rearrange("p (a t) -> p t a", t=4))
+
+        def lay_planes(rows):
+            for row in rows:
+                j, o = divmod(row, O)
+                first = RAW + 16 * o + j
+                nc.sync.dma_start(ksp[4 * o + j:P:32, :].bitcast(I32), ksr[first:first + 13:4, :].bitcast(I32))
+
+        vsw = reuse.tile([P, T], F32, name="vsw", offset=2 * WINDOW, align_bytes=64)
+        nc.vector.memset(vsw[0:VS_ROW, :], 0.0)
+        nc.sync.dma_start(vsw[VS_ROW:P, :], vs[0:1, :])
+        lay_planes(range(0, AHEAD))
+        kw1 = reuse.tile([P, T], I32, name="kw1", offset=WINDOW, align_bytes=64)
+        nc.sync.dma_start(kw1[:, 0:EARLY], words(1)[:, 0:EARLY])
+        nc.sync.dma_start(kw1[:, EARLY:T], words(1)[:, EARLY:T])
+        kw = [kw0, kw1]
+        lay_planes(range(AHEAD, 4 * O))
+
+        def turn(places, name, bank):
+            turned = psum.tile([P, 4, P], F32, name=name + "t", tag=bank)
             for t in range(4):
-                nc.tensor.transpose(turned[:, t, :], laid[:, t, :].bitcast(F32), ident[:])
-            cols = keep.tile([P, 4], F32, name=name + "c%d" % g)
-            nc.scalar.copy(cols[:], turned[:, :, ROW])
+                nc.tensor.transpose(turned[:, t, :], places[:, t, :], ident[:])
+            return turned
+
+        def columns(places, row, name, bank):
+            cols = keep.tile([P, 4], F32, name=name + "c")
+            nc.scalar.copy(cols[:], turn(places, name, bank)[:, :, row])
             return cols
 
-        def whole_list(ap):
-            return ap.rearrange("p g t (a r) -> p g a t r", r=4)
+        def every_fourth(ap):
+            return ap.rearrange("p (c t) -> p t c", t=4)
 
-        kg0 = keep.tile([P, G, 4, P], U32, name="kg0", align_bytes=64)
+        kbg = keep.tile([P, N], F32, name="kbg", align_bytes=64)
+        kb0 = keep.tile([P, 4, P], F32, name="kb0", align_bytes=64)
+        nc.scalar.activation(kbg[:], kbw[:].indirect(offsets[:]), ACT.Copy)
+        nc.scalar.activation(kb0[:].rearrange("p t (a r) -> p t a r", r=4),
+                             kbg[:, 0:PASS].rearrange("p (a t r) -> p t a r", t=4, r=4), ACT.Copy)
+        kbc = [None, columns(every_fourth(kbg[:, PASS:N]), KB_ROW, "kb1", "turn1")]
+        kbc[0] = columns(kb0[:], KB_ROW, "kb0", "turn0")
+        vw = [reuse.tile([P, T], F32, name="vw0", offset=5 * WINDOW, align_bytes=64)]
+        nc.sync.dma_start(vw[0][:], vT[0:P, :])
+        vsg = keep.tile([P, N], F32, name="vsg", align_bytes=64)
+        vs0 = keep.tile([P, 4, P], F32, name="vs0", align_bytes=64)
+        nc.scalar.activation(vsg[:], vsw[:].indirect(offsets[:]), ACT.Copy)
+        nc.scalar.activation(vs0[:].rearrange("p t (a r) -> p t a r", r=4),
+                             vsg[:, 0:PASS].rearrange("p (a t r) -> p t a r", t=4, r=4), ACT.Copy)
+
+        kg0 = reuse.tile([P, G, 4, P], U32, name="kg0", offset=3 * WINDOW, align_bytes=64)
         kg = [[kg0[:, g] for g in range(G)],
               [keep.tile([P, 4, P], U32, name="kg1%d" % g, align_bytes=64)[:] for g in range(G)]]
 
-        kbg = keep.tile([P, G, 4, P], U32, name="kbg", align_bytes=64)
-        nc.vector.tensor_copy(whole_list(kbg[:]), kbw[:].bitcast(U32).indirect(offsets[:]))
-        kbc = [turn(kbg[:, g], "kb", g) for g in range(G)]
-        vw = [keep.tile([P, T], F32, name="vw0", tag="bias", align_bytes=64)]
-        load_window(vw[0], vT[0:P, :])
-        nc.vector.tensor_copy(whole_list(kg0[:]), kw[0][:].bitcast(U32).indirect(offsets[:]))
-        vsg0 = reuse.tile([P, 4, P], U32, name="vsg0", offset=4 * T - 4 * DV, align_bytes=64)
-        nc.vector.tensor_copy(by_block(vsg0[:]), vsw[:].bitcast(U32).indirect(slots(0)))
-        vsc = [turn(vsg0, "vs", 0)]
-        vw.append(reuse.tile([P, T], F32, name="vw1", offset=0, align_bytes=64))
-        ogt = reuse.tile([P, DV], F32, name="ogt", offset=4 * T, align_bytes=64)
-        nc.sync.dma_start(vw[1][:, 0:EARLY], vT[P:2 * P, 0:EARLY])
-        nc.sync.dma_start(ogt[:], og[0])
-        nc.sync.dma_start(vw[1][:, EARLY:T], vT[P:2 * P, EARLY:T])
-        for g in range(G):
-            nc.vector.tensor_copy(by_block(kg[1][g]), window(kw[1], g).bitcast(U32).indirect(slots(g)))
-        vsg1 = keep.tile([P, 4, P], U32, name="vsg1", tag="keys1", align_bytes=64)
-        nc.vector.tensor_copy(by_block(vsg1[:]), vsw[:].bitcast(U32).indirect(slots(1)))
+        def gather_keys(o):
+            for g in range(G):
+                window = kw[o][:, 0:EARLY] if g == 0 else kw[o][:]
+                nc.vector.tensor_copy(slot_order(kg[o][g], g), window.bitcast(U32).indirect(slots(g * PASS, PASS)))
 
-        rel = keep.tile([P, G, 4, NQ], F32, name="rel")
+        gather_keys(0)
+        vw.append(reuse.tile([P, T], F32, name="vw1", offset=0, align_bytes=64))
+        nc.sync.dma_start(vw[1][:, 0:EARLY], vT[P:2 * P, 0:EARLY])
+        nc.sync.dma_start(vw[1][:, EARLY:T], vT[P:2 * P, EARLY:T])
+        gather_keys(1)
+        ogt = reuse.tile([P, DV], F32, name="ogt", offset=WINDOW, align_bytes=64)
+        nc.sync.dma_start(ogt[:], og[0])
+
+        rel = reuse.tile([P, G, 4, NQ], F32, name="rel", offset=4 * WINDOW, align_bytes=64)
         prob = keep.tile([P, G, 4, NQ], F32, name="prob")
+        banks = [["score0", "score1", "score2", "score3"], ["turn0", "turn1", "vt0", "vt1"]]
         for g in range(G):
-            score = [psum.tile([P, NQ], F32, name="score%d%d" % (g, t), tag="turn1" if (g, t) == (1, 3) else "score%d" % t) for t in range(4)]
+            score = [psum.tile([P, NQ], F32, name="score%d%d" % (g, t), tag=banks[g][t]) for t in range(4)]
             for t in range(4):
                 for o in range(O):
                     first = g * PASS + t * P
                     nc.tensor.matmul_mx(
                         out=score[t][:],
-                        lhsT=kg[o][g][:, t, :].bitcast(X4), lhsT_scale=ksp[:, o, first:first + P],
-                        rhs=qw[:, o, :].bitcast(X4), rhs_scale=ksp[:, o, N:N + NQ],
+                        lhsT=kg[o][g][:, t, :].bitcast(X4), lhsT_scale=ksp[4 * o:P, first:first + P],
+                        rhs=qw[:, o, :].bitcast(X4), rhs_scale=ksp[4 * o:P, N:N + NQ],
                         start=(o == 0), stop=(o == O - 1))
             for t in range(4):
-                nc.scalar.activation(rel[:, g, t, :], score[t][:], ACT.Relu, bias=kbc[g][:, t:t + 1])
+                if g == 0:
+                    nc.scalar.activation(rel[:, g, t, :], score[t][:], ACT.Relu, bias=kbc[g][:, t:t + 1])
+                else:
+                    nc.vector.tensor_scalar(rel[:, g, t, :], score[t][:], kbc[g][:, t:t + 1], 0.0, ALU.add, ALU.max)
             nc.scalar.activation(prob[:, g], rel[:, g], ACT.Square)
-        vsc.append(turn(vsg1, "vs", 1))
+        vst = [turn(vs0[:], "vs0", "score2"), turn(every_fourth(vsg[:, PASS:N]), "vs1", "score3")]
 
-        vin = [keep.tile([P, G, P, 4], BF16, name="vin%d" % h, tag="vin%d" % h, align_bytes=64) for h in range(H)]
+        vin = [keep.tile([P, G, P, 4], BF16, name="vin%d" % h, align_bytes=64) for h in range(H)]
         vq = [None, keep.tile([P, G, P], U32, name="vq1", align_bytes=64)]
         vqs = [keep.tile([P, G, P], U8, name="vqs%d" % h, align_bytes=64) for h in range(H)]
 
-        def gather_values(h, g):
-            vb = keep.tile([P, 2, P, 2], BF16, name="vb%d%d" % (h, g), align_bytes=64)
-            nc.vector.tensor_copy(vb[:].rearrange("p u (a r) s -> p a u s r", r=4), window(vw[h], g).indirect(slots(g)))
+        def gather_values(h, g, window, share):
+            vb = reuse.tile([P, PASS], BF16, name="vb%d%d" % (h, g), align_bytes=64,
+                            offset=WINDOW + 4 * DV if (h, g) == (0, 0) else 4 * WINDOW + (G * h + g) * 2 * PASS)
+            if g == 0:
+                nc.vector.tensor_copy(vb[:].rearrange("p (u a r s) -> p a u s r", u=2, r=4, s=2), window.indirect(slots(0, PASS)))
+                return vb[:].bitcast(F32).rearrange("p (u c) -> p u c", u=2)
+            nc.scalar.activation(vb[:, 0:share], window.indirect(slots(PASS, share)), ACT.Copy)
+            if share < PASS:
+                nc.vector.tensor_copy(vb[:, share:PASS], window.indirect(slots(PASS + share, PASS - share)))
+            return vb[:].bitcast(F32).rearrange("p (c u) -> p u c", u=2)
+
+        def turn_values(h, g, pairs, copy):
             turned = psum.tile([P, 2, P], F32, name="vt%d%d" % (h, g), tag="vt%d" % g)
             for u in range(2):
-                nc.tensor.transpose(turned[:, u, :], vb[:, u].rearrange("p c s -> p (c s)").bitcast(F32), ident[:])
-            nc.scalar.copy(vin[h][:, g].bitcast(F32), turned[:].rearrange("p u e -> p e u"))
+                nc.tensor.transpose(turned[:, u, :], pairs[:, u, :], ident[:])
+            copy(vin[h][:, g].bitcast(F32), turned[:].rearrange("p u e -> p e u"))
 
         def quantize(codes, scales, values):
             nc.vector.quantize_mx(out=codes.rearrange("p g c -> p (g c)").bitcast(X4), scales=scales.rearrange("p g c -> p (g c)"),
                                   in_=values.rearrange("p g c t -> p (g c t)"))
 
-        def quantize_values(h, g):
-            quantize(vq[h][:, g:g + 1], vqs[h][:, g:g + 1], vin[h][:, g:g + 1])
-
-        wq = keep.tile([P, G, NQ], U32, name="wq", align_bytes=64)
         wqs = keep.tile([P, G, NQ], U8, name="wqs", align_bytes=64)
-
-        def weigh(g, wb):
-            nc.vector.tensor_tensor(wb.rearrange("p (c i) t -> p c t i", i=2),
-                                    prob[:, g].rearrange("p t (c i) -> p c t i", i=2),
-                                    vsc[g][:].unsqueeze(1).unsqueeze(3).to_broadcast([P, NQ // 2, 4, 2]), ALU.mult)
-
-        gather_values(0, 0)
-        gather_values(0, 1)
-        wb = keep.tile([P, G, NQ, 4], BF16, name="wb", tag="bias", align_bytes=64)
+        wb = keep.tile([P, G, NQ, 4], BF16, name="wb", align_bytes=64)
         for g in range(G):
-            weigh(g, wb[:, g])
+            nc.vector.tensor_tensor(wb[:, g].rearrange("p (c i) t -> p c t i", i=2),
+                                    prob[:, g].rearrange("p t (c i) -> p c t i", i=2),
+                                    vst[g][:, :, VS_ROW].unsqueeze(1).unsqueeze(3).to_broadcast([P, NQ // 2, 4, 2]), ALU.mult)
+        pairs = [gather_values(0, g, vw[0][:], PASS) for g in range(G)]
+        for g in range(G):
+            turn_values(0, g, pairs[g], nc.scalar.copy)
+        wq = reuse.tile([P, G, NQ], U32, name="wq", offset=5 * WINDOW, align_bytes=64)
         quantize(wq[:], wqs[:], wb[:])
 
-        back = psum.tile([P, P], F32, name="back", tag="score2")
+        back = psum.tile([P, P], F32, name="back", tag="score0")
         for i in range(4 * G):
             nc.tensor.matmul(back[:], prob[:, i // 4, i % 4, :], ident[:], start=(i == 0), stop=(i == 4 * G - 1), is_transpose=True)
-        spare = keep.tile([P, P], F32, name="spare")
+        spare = reuse.tile([P, P], F32, name="spare", offset=5 * WINDOW + 4 * G * NQ, align_bytes=64)
         total = keep.tile([P, 1], F32, name="total")
         nc.scalar.activation(spare[:], back[:], ACT.Copy, bias=1.0 / P, accum_out=total[:])
 
+        pairs = [gather_values(1, 0, vw[1][:, 0:EARLY], PASS), gather_values(1, 1, vw[1][:], SHARE)]
+        inv = reuse.tile([P, 1], F32, name="inv", offset=0, align_bytes=64)
+        turn_values(1, 0, pairs[0], nc.vector.tensor_copy)
+        vq[0] = reuse.tile([P, G, P], U32, name="vq0", offset=2048, align_bytes=64)
+        quantize(vq[0][:], vqs[0][:], vin[0][:])
         half = keep.tile([P, DV], F32, name="half")
         gate = keep.tile([P, DV], F32, name="gate")
         nc.scalar.activation(half[:], ogt[:], ACT.Tanh, scale=0.5)
         nc.scalar.activation(gate[:], half[:], ACT.Copy, scale=0.5, bias=0.5)
-        gather_values(1, 0)
-        gather_values(1, 1)
-        inv = reuse.tile([P, 1], F32, name="inv", offset=0, align_bytes=64)
-        vq[0] = reuse.tile([P, G, P], U32, name="vq0", offset=2048, align_bytes=64)
+        turn_values(1, 1, pairs[1], nc.scalar.copy)
+        quantize(vq[1][:, 0:1], vqs[1][:, 0:1], vin[1][:, 0:1])
         nc.vector.reciprocal(inv[:], total[:])
-        quantize(vq[0][:], vqs[0][:], vin[0][:])
-        quantize_values(1, 0)
-        quantize_values(1, 1)
-        res = keep.tile([P, DV], F32, name="res", tag="vin1", align_bytes=64)
+        res = keep.tile([P, DV], F32, name="res", align_bytes=64)
 
         def finish(h):
-            y = psum.tile([P, P], F32, name="y%d" % h, tag="score%d" % h)
+            y = psum.tile([P, P], F32, name="y%d" % h, tag="turn%d" % h)
             for g in range(G):
                 nc.tensor.matmul_mx(out=y[:], lhsT=wq[:, g].bitcast(X4), lhsT_scale=wqs[:, g],
                                     rhs=vq[h][:, g].bitcast(X4), rhs_scale=vqs[h][:, g],
@@ -213,4 +239,5 @@ def tile_attend_rel2_kb_gate_srtq128n1024t4096_kernel(tc, q_words, q_scales, k_w
             nc.sync.dma_start(out[0][:, cols], res[:, cols])
 
         finish(0)
+        quantize(vq[1][:, 1:2], vqs[1][:, 1:2], vin[1][:, 1:2])
         finish(1)

from contextlib import ExitStack

import concourse.mybir as mybir

N, T, D, DV, NQ = 1024, 4096, 1024, 256, 128
FLOPS = 2 * NQ * N * D + 2 * NQ * N * DV
BYTES = D * T + D * T // 32 + 4 * DV * T + 2 * 4 * T + D * NQ + D * NQ // 32 + 2 * 4 * NQ * DV + 2 * 8 * N

F32 = mybir.dt.float32
BF16 = mybir.dt.bfloat16
I32 = mybir.dt.int32
U32 = mybir.dt.uint32
U16 = mybir.dt.uint16
U8 = mybir.dt.uint8
X4 = mybir.dt.float8_e4m3fn_x4
ACT = mybir.ActivationFunctionType
ALU = mybir.AluOpType

P = 128
PASS = 512
G = N // PASS
O = D // PASS
H = DV // P
KB_ROW = P - 1
VS_ROW = P - 1
EARLY = T - (N - PASS)
SHARE = 352
RAW = 32
RAW_END = RAW + 32
ZEROED = 1408
AHEAD = 3
WINDOW = 4 * T


def tile_attend_rel2_kb_gate_srtq128n1024t4096_kernel(tc, q_words, q_scales, k_words, k_scales, vT, vs, kb, og, offs, out):
    nc = tc.nc
    with ExitStack() as ctx:
        keep = ctx.enter_context(tc.tile_pool(name="keep", bufs=1))
        reuse = ctx.enter_context(tc.tile_pool(name="reuse", bufs=1))
        psum = ctx.enter_context(tc.psum_pool(name="psum", bufs=1))

        def words(o):
            return k_words[o].rearrange("g t r -> g (t r)").bitcast(I32)

        offsets = keep.tile([P, N // 16], U16, name="offsets")
        kbw = reuse.tile([P, T], F32, name="kbw", offset=5 * WINDOW, align_bytes=64)
        kw0 = reuse.tile([P, T], I32, name="kw0", offset=0, align_bytes=64)
        ramp = keep.tile([P, P], F32, name="ramp")
        kbs = keep.tile([P, 32], F32, name="kbs")
        ksw = reuse.tile([P, T], U8, name="ksw", offset=3 * WINDOW, align_bytes=64)
        qw = keep.tile([P, O, NQ], I32, name="qw", align_bytes=64)
        ksr = keep.tile([P, N + NQ], U8, name="ksr", align_bytes=64)
        ksp = keep.tile([P, N + NQ], U8, name="ksp", align_bytes=64)
        ident = keep.tile([P, P], F32, name="ident")

        def slots(first, count):
            return offsets[:, first // 16:(first + count) // 16]

        def slot_order(ap, g):
            if g == 0:
                return ap.rearrange("p t (a r) -> p a t r", r=4)
            return ap.rearrange("p t c -> p c t")

        nc.gpsimd.iota(ramp[:], [[1, P]], base=0, channel_multiplier=-1, allow_small_or_imprecise_dtypes=True)
        nc.vector.memset(ksw[0:RAW, :].bitcast(I32), 0)
        nc.vector.memset(ksw[RAW_END:P, :].bitcast(I32), 0)
        nc.vector.tensor_scalar(ident[:], ramp[:], 0.0, None, ALU.is_equal)
        nc.vector.memset(ksp[:].bitcast(I32), 0)
        nc.vector.memset(kbw[0:KB_ROW, 0:ZEROED], 0.0)

        nc.sync.dma_start(ksw[RAW:RAW_END, :].bitcast(I32), k_scales.rearrange("o f t -> (o f) t").bitcast(I32))
        nc.sync.dma_start(offsets[:], offs)
        nc.sync.dma_start(kbs[:], kb[:, 0:32])
        nc.sync.dma_start(kbw[KB_ROW:P, :], kb[0:1, :])
        nc.sync.dma_start(ksr[RAW:RAW_END, N:N + NQ].bitcast(I32), q_scales[0].rearrange("o f q -> (o f) q").bitcast(I32))
        nc.sync.dma_start(qw[:], q_words[0].rearrange("o g q r -> g o (q r)").bitcast(I32))
        nc.sync.dma_start(kw0[:], words(0))

        nc.scalar.activation(kbw[0:KB_ROW, ZEROED:T].rearrange("p (a b) -> p a b", b=32),
                             kbs[0:KB_ROW, :].unsqueeze(1).to_broadcast([KB_ROW, (T - ZEROED) // 32, 32]), ACT.Copy)

        ksg = reuse.tile([P, N], U8, name="ksg", offset=2 * WINDOW - PASS, align_bytes=64)
        for g in (1, 0):
            nc.vector.tensor_copy(ksg[:, g * PASS:(g + 1) * PASS], ksw[:].indirect(slots(g * PASS, PASS)))
        nc.vector.tensor_copy(ksr[:, PASS:N].rearrange("p (t c) -> p t c", t=4),
                              ksg[:, PASS:N].rearrange("p (c t) -> p t c", t=4))
        nc.vector.tensor_copy(ksr[RAW:RAW_END, 0:PASS].bitcast(I32).rearrange("p (t a) -> p t a", t=4),
                              ksg[RAW:RAW_END, 0:PASS].bitcast(I32).rearrange("p (a t) -> p t a", t=4))

        def lay_planes(rows):
            for row in rows:
                j, o = divmod(row, O)
                first = RAW + 16 * o + j
                nc.sync.dma_start(ksp[4 * o + j:P:32, :].bitcast(I32), ksr[first:first + 13:4, :].bitcast(I32))

        vsw = reuse.tile([P, T], F32, name="vsw", offset=2 * WINDOW, align_bytes=64)
        nc.vector.memset(vsw[0:VS_ROW, :], 0.0)
        nc.sync.dma_start(vsw[VS_ROW:P, :], vs[0:1, :])
        lay_planes(range(0, AHEAD))
        kw1 = reuse.tile([P, T], I32, name="kw1", offset=WINDOW, align_bytes=64)
        nc.sync.dma_start(kw1[:, 0:EARLY], words(1)[:, 0:EARLY])
        nc.sync.dma_start(kw1[:, EARLY:T], words(1)[:, EARLY:T])
        kw = [kw0, kw1]
        lay_planes(range(AHEAD, 4 * O))

        def turn(places, name, bank):
            turned = psum.tile([P, 4, P], F32, name=name + "t", tag=bank)
            for t in range(4):
                nc.tensor.transpose(turned[:, t, :], places[:, t, :], ident[:])
            return turned

        def columns(places, row, name, bank):
            cols = keep.tile([P, 4], F32, name=name + "c")
            nc.scalar.copy(cols[:], turn(places, name, bank)[:, :, row])
            return cols

        def every_fourth(ap):
            return ap.rearrange("p (c t) -> p t c", t=4)

        kbg = keep.tile([P, N], F32, name="kbg", align_bytes=64)
        kb0 = keep.tile([P, 4, P], F32, name="kb0", align_bytes=64)
        nc.scalar.activation(kbg[:], kbw[:].indirect(offsets[:]), ACT.Copy)
        nc.scalar.activation(kb0[:].rearrange("p t (a r) -> p t a r", r=4),
                             kbg[:, 0:PASS].rearrange("p (a t r) -> p t a r", t=4, r=4), ACT.Copy)
        kbc = [None, columns(every_fourth(kbg[:, PASS:N]), KB_ROW, "kb1", "turn1")]
        kbc[0] = columns(kb0[:], KB_ROW, "kb0", "turn0")
        vw = [reuse.tile([P, T], F32, name="vw0", offset=5 * WINDOW, align_bytes=64)]
        nc.sync.dma_start(vw[0][:], vT[0:P, :])
        vsg = keep.tile([P, N], F32, name="vsg", align_bytes=64)
        vs0 = keep.tile([P, 4, P], F32, name="vs0", align_bytes=64)
        nc.scalar.activation(vsg[:], vsw[:].indirect(offsets[:]), ACT.Copy)
        nc.scalar.activation(vs0[:].rearrange("p t (a r) -> p t a r", r=4),
                             vsg[:, 0:PASS].rearrange("p (a t r) -> p t a r", t=4, r=4), ACT.Copy)

        kg0 = reuse.tile([P, G, 4, P], U32, name="kg0", offset=3 * WINDOW, align_bytes=64)
        kg = [[kg0[:, g] for g in range(G)],
              [keep.tile([P, 4, P], U32, name="kg1%d" % g, align_bytes=64)[:] for g in range(G)]]

        def gather_keys(o):
            for g in range(G):
                window = kw[o][:, 0:EARLY] if g == 0 else kw[o][:]
                nc.vector.tensor_copy(slot_order(kg[o][g], g), window.bitcast(U32).indirect(slots(g * PASS, PASS)))

        gather_keys(0)
        vw.append(reuse.tile([P, T], F32, name="vw1", offset=0, align_bytes=64))
        nc.sync.dma_start(vw[1][:, 0:EARLY], vT[P:2 * P, 0:EARLY])
        nc.sync.dma_start(vw[1][:, EARLY:T], vT[P:2 * P, EARLY:T])
        gather_keys(1)
        ogt = reuse.tile([P, DV], F32, name="ogt", offset=WINDOW, align_bytes=64)
        nc.sync.dma_start(ogt[:], og[0])

        rel = reuse.tile([P, G, 4, NQ], F32, name="rel", offset=4 * WINDOW, align_bytes=64)
        prob = keep.tile([P, G, 4, NQ], F32, name="prob")
        banks = [["score0", "score1", "score2", "score3"], ["turn0", "turn1", "vt0", "vt1"]]
        for g in range(G):
            score = [psum.tile([P, NQ], F32, name="score%d%d" % (g, t), tag=banks[g][t]) for t in range(4)]
            for t in range(4):
                for o in range(O):
                    first = g * PASS + t * P
                    nc.tensor.matmul_mx(
                        out=score[t][:],
                        lhsT=kg[o][g][:, t, :].bitcast(X4), lhsT_scale=ksp[4 * o:P, first:first + P],
                        rhs=qw[:, o, :].bitcast(X4), rhs_scale=ksp[4 * o:P, N:N + NQ],
                        start=(o == 0), stop=(o == O - 1))
            for t in range(4):
                if g == 0:
                    nc.scalar.activation(rel[:, g, t, :], score[t][:], ACT.Relu, bias=kbc[g][:, t:t + 1])
                else:
                    nc.vector.tensor_scalar(rel[:, g, t, :], score[t][:], kbc[g][:, t:t + 1], 0.0, ALU.add, ALU.max)
            nc.scalar.activation(prob[:, g], rel[:, g], ACT.Square)
        vst = [turn(vs0[:], "vs0", "score2"), turn(every_fourth(vsg[:, PASS:N]), "vs1", "score3")]

        vin = [keep.tile([P, G, P, 4], BF16, name="vin%d" % h, align_bytes=64) for h in range(H)]
        vq = [None, keep.tile([P, G, P], U32, name="vq1", align_bytes=64)]
        vqs = [keep.tile([P, G, P], U8, name="vqs%d" % h, align_bytes=64) for h in range(H)]

        def gather_values(h, g, window, share):
            vb = reuse.tile([P, PASS], BF16, name="vb%d%d" % (h, g), align_bytes=64,
                            offset=WINDOW + 4 * DV if (h, g) == (0, 0) else 4 * WINDOW + (G * h + g) * 2 * PASS)
            if g == 0:
                nc.vector.tensor_copy(vb[:].rearrange("p (u a r s) -> p a u s r", u=2, r=4, s=2), window.indirect(slots(0, PASS)))
                return vb[:].bitcast(F32).rearrange("p (u c) -> p u c", u=2)
            nc.scalar.activation(vb[:, 0:share], window.indirect(slots(PASS, share)), ACT.Copy)
            if share < PASS:
                nc.vector.tensor_copy(vb[:, share:PASS], window.indirect(slots(PASS + share, PASS - share)))
            return vb[:].bitcast(F32).rearrange("p (c u) -> p u c", u=2)

        def turn_values(h, g, pairs, copy):
            turned = psum.tile([P, 2, P], F32, name="vt%d%d" % (h, g), tag="vt%d" % g)
            for u in range(2):
                nc.tensor.transpose(turned[:, u, :], pairs[:, u, :], ident[:])
            copy(vin[h][:, g].bitcast(F32), turned[:].rearrange("p u e -> p e u"))

        def quantize(codes, scales, values):
            nc.vector.quantize_mx(out=codes.rearrange("p g c -> p (g c)").bitcast(X4), scales=scales.rearrange("p g c -> p (g c)"),
                                  in_=values.rearrange("p g c t -> p (g c t)"))

        wqs = keep.tile([P, G, NQ], U8, name="wqs", align_bytes=64)
        wb = keep.tile([P, G, NQ, 4], BF16, name="wb", align_bytes=64)
        for g in range(G):
            nc.vector.tensor_tensor(wb[:, g].rearrange("p (c i) t -> p c t i", i=2),
                                    prob[:, g].rearrange("p t (c i) -> p c t i", i=2),
                                    vst[g][:, :, VS_ROW].unsqueeze(1).unsqueeze(3).to_broadcast([P, NQ // 2, 4, 2]), ALU.mult)
        pairs = [gather_values(0, g, vw[0][:], PASS) for g in range(G)]
        for g in range(G):
            turn_values(0, g, pairs[g], nc.scalar.copy)
        wq = reuse.tile([P, G, NQ], U32, name="wq", offset=5 * WINDOW, align_bytes=64)
        quantize(wq[:], wqs[:], wb[:])

        back = psum.tile([P, P], F32, name="back", tag="score0")
        for i in range(4 * G):
            nc.tensor.matmul(back[:], prob[:, i // 4, i % 4, :], ident[:], start=(i == 0), stop=(i == 4 * G - 1), is_transpose=True)
        spare = reuse.tile([P, P], F32, name="spare", offset=5 * WINDOW + 4 * G * NQ, align_bytes=64)
        total = keep.tile([P, 1], F32, name="total")
        nc.scalar.activation(spare[:], back[:], ACT.Copy, bias=1.0 / P, accum_out=total[:])

        pairs = [gather_values(1, 0, vw[1][:, 0:EARLY], PASS), gather_values(1, 1, vw[1][:], SHARE)]
        inv = reuse.tile([P, 1], F32, name="inv", offset=0, align_bytes=64)
        turn_values(1, 0, pairs[0], nc.vector.tensor_copy)
        vq[0] = reuse.tile([P, G, P], U32, name="vq0", offset=2048, align_bytes=64)
        quantize(vq[0][:], vqs[0][:], vin[0][:])
        half = keep.tile([P, DV], F32, name="half")
        gate = keep.tile([P, DV], F32, name="gate")
        nc.scalar.activation(half[:], ogt[:], ACT.Tanh, scale=0.5)
        nc.scalar.activation(gate[:], half[:], ACT.Copy, scale=0.5, bias=0.5)
        turn_values(1, 1, pairs[1], nc.scalar.copy)
        quantize(vq[1][:, 0:1], vqs[1][:, 0:1], vin[1][:, 0:1])
        nc.vector.reciprocal(inv[:], total[:])
        res = keep.tile([P, DV], F32, name="res", align_bytes=64)

        def finish(h):
            y = psum.tile([P, P], F32, name="y%d" % h, tag="turn%d" % h)
            for g in range(G):
                nc.tensor.matmul_mx(out=y[:], lhsT=wq[:, g].bitcast(X4), lhsT_scale=wqs[:, g],
                                    rhs=vq[h][:, g].bitcast(X4), rhs_scale=vqs[h][:, g],
                                    start=(g == 0), stop=(g == G - 1))
            cols = slice(h * P, (h + 1) * P)
            nc.vector.scalar_tensor_tensor(res[:, cols], y[:], inv[:], gate[:, cols], ALU.mult, ALU.mult)
            nc.sync.dma_start(out[0][:, cols], res[:, cols])

        finish(0)
        quantize(vq[1][:, 1:2], vqs[1][:, 1:2], vin[1][:, 1:2])
        finish(1)
